import numpy as np
import ml_dtypes


def mxq(x, axis, fmt="e4m3"):
    dtype, down = {"e4m3": (ml_dtypes.float8_e4m3fn, 7), "e5m2": (ml_dtypes.float8_e5m2, 14)}[fmt]
    v = np.moveaxis(np.asarray(x, np.float32).astype(ml_dtypes.bfloat16).astype(np.float64), axis, -1)
    blocks = v.reshape(v.shape[:-1] + (-1, 32))
    amax = np.abs(blocks).max(-1, keepdims=True)
    byte = np.maximum(np.where(amax > 0, np.frexp(amax)[1] - 1 + 127, 0) - down, 1)
    scale = np.exp2(byte - 127.0)
    codes = (blocks / scale).astype(np.float32).astype(dtype).astype(np.float64)
    return np.moveaxis((codes * scale).reshape(v.shape), -1, axis)


WIDE = False


def mx_kscale(k):
    if not WIDE:
        return np.ones(k)
    levels = np.array([10, -10, 5, -5, 0])
    if k % 512:
        return np.exp2(np.random.permutation(np.resize(levels, k // 32))).repeat(32)
    a = np.empty((k // 512, 16))
    for p in range(k // 512):
        a[p, :8] = np.random.permutation(np.resize(levels, 8))
        for g in range(8):
            far = levels[np.abs(levels - a[p, g]) >= 10]
            a[p, g + 8] = far[np.random.randint(len(far))]
    return np.exp2(a.ravel()).repeat(32)


def f64(x):
    return np.asarray(x).astype(np.float64)


def striped(idx):
    return np.tile(idx.reshape(-1, 16).T, (8, 1)).astype(np.uint16)


def unstriped(offs):
    return offs[:16].T.reshape(-1).astype(np.int64)


E2M1 = np.array([0.0, 0.5, 1.0, 1.5, 2.0, 3.0, 4.0, 6.0, -0.0, -0.5, -1.0, -1.5, -2.0, -3.0, -4.0, -6.0])


def pack_weight(w, fmt):
    k, n = w.shape
    w = f64(np.asarray(w, np.float32).astype(ml_dtypes.bfloat16)).reshape(k // 32, 32, n)
    amax = np.abs(w).max(1)
    if fmt == "e4m3":
        byte = np.frexp(amax)[1] - 1 + 127 - 7
    else:
        mant, ex = np.frexp(amax / 6.0)
        byte = np.where(mant > 0.5, ex, ex - 1) + 127
    byte = np.clip(np.where(amax > 0, byte, 1), 1, 254)
    scaled = (w * np.exp2(127.0 - byte)[:, None, :]).reshape(k, n).astype(np.float32)
    by_word = np.ascontiguousarray(scaled.reshape(k // 512, 128, 4, n).transpose(0, 1, 3, 2))
    if fmt == "e4m3":
        words = by_word.astype(ml_dtypes.float8_e4m3fn).view(np.uint8)
    else:
        c = by_word.astype(ml_dtypes.float4_e2m1fn).view(np.uint8) & 0xF
        words = (c[..., 0::2] | (c[..., 1::2] << 4)).reshape(k // 512, 128, 2 * n)
    return np.ascontiguousarray(words), np.ascontiguousarray(byte.astype(np.uint8).reshape(k // 512, 16, n))


def unpack_weight(words, scales, fmt):
    g, _, n = scales.shape
    words = np.ascontiguousarray(words).reshape(g, 128, n, -1)
    if fmt == "e4m3":
        vals = words.view(ml_dtypes.float8_e4m3fn).astype(np.float64)
    else:
        nib = np.empty((g, 128, n, 4), np.uint8)
        nib[..., 0::2] = words & 0xF
        nib[..., 1::2] = words >> 4
        vals = E2M1[nib]
    vals = vals * np.repeat(np.exp2(scales.astype(np.float64) - 127.0), 8, axis=1)[..., None]
    return vals.transpose(0, 1, 3, 2).reshape(g * 512, n)


def planes(y):
    n, m = y.shape
    v = y.astype(np.float32).astype(ml_dtypes.bfloat16).astype(np.float64).reshape(n // 32, 32, m)
    top = np.abs(v).max(1)
    byte = np.clip(np.where(top > 0, np.frexp(top)[1] - 1 + 127 - 7, 1), 1, 254)
    codes = (v * np.exp2(127.0 - byte)[:, None, :]).reshape(n, m).astype(np.float32).astype(ml_dtypes.float8_e4m3fn).view(np.uint8)
    words = codes.reshape(n // 512, 128, 4, m).transpose(0, 1, 3, 2)
    return np.ascontiguousarray(words), np.ascontiguousarray(byte.astype(np.uint8).reshape(n // 512, 16, m))


def relu(v):
    return np.maximum(v, 0.0)


K, T, E, C, H, N = 512, 1024, 16, 128, 512, 512


def by_expert(wq, xq):
    return np.concatenate([wq[e].T @ xq[:, e * C:(e + 1) * C] for e in range(E)], axis=1)


def setup_inputs():
    n = np.random.standard_normal
    s = mx_kscale(K)
    u = mx_kscale(H)
    first = np.random.permutation(np.repeat(np.arange(E), T // E))
    second = (first + 1 + np.random.permutation(np.repeat(np.arange(E - 1), -(-T // (E - 1)))[:T])) % E
    while np.bincount(second, minlength=E).max() != T // E:
        load = np.bincount(second, minlength=E); hi, lo = int(load.argmax()), int(load.argmin())
        t = np.flatnonzero((second == hi) & (first != lo))[0]; second[t] = lo
    slot_token = np.empty(E * C, np.int64); pos = np.empty((2, T), np.int64); fill = np.zeros(E, np.int64)
    place = np.stack([np.random.permutation(C) for _ in range(E)])
    for r, deal in enumerate((first, second)):
        for t in np.random.permutation(T):
            e = deal[t]; j = e * C + place[e, fill[e]]; fill[e] += 1; slot_token[j] = t; pos[r, t] = j
    g = np.random.uniform(0.2, 0.8, T)
    x = pack_weight(n((K, T)) * s[:, None], "e4m3")
    w1 = pack_weight(n((K, H)) / np.sqrt(K) / s[:, None], "e4m3")
    w3 = pack_weight(n((K, H)) / np.sqrt(K) / s[:, None] * u, "e4m3")
    w2 = [pack_weight(m, "e2m1") for m in n((E, H, N)) / np.sqrt(H) / u[None, :, None]]
    return {
        "x_words": x[0],
        "x_scales": x[1],
        "w1_words": w1[0],
        "w1_scales": w1[1],
        "w3_words": w3[0],
        "w3_scales": w3[1],
        "w2_words": np.stack([m[0] for m in w2]),
        "w2_scales": np.stack([m[1] for m in w2]),
        "gate": np.stack([np.tile(g, (128, 1)), np.tile(1.0 - g, (128, 1))]).astype(np.float32),
        "offs": striped(slot_token),
        "pos1": striped(pos[0]),
        "pos2": striped(pos[1]),
    }


def reference(x_words, x_scales, w1_words, w1_scales, w3_words, w3_scales, w2_words, w2_scales, gate, offs, pos1, pos2):
    w1 = unpack_weight(w1_words, w1_scales, "e4m3")
    w3 = unpack_weight(w3_words, w3_scales, "e4m3")
    w2 = np.stack([unpack_weight(w2_words[e], w2_scales[e], "e2m1") for e in range(E)])
    idx = unstriped(offs)
    x = unpack_weight(x_words, x_scales, "e4m3")
    h = relu(w1.T @ x) * (w3.T @ x)
    y = by_expert(w2, mxq(h[:, idx], 0, "e4m3"))
    out = sum(f64(gate[r, :1]) * y[:, unstriped(p)] for r, p in enumerate((pos1, pos2)))
    out_0 = out
    return (out_0,) + planes(out_0)

@@ -1,0 +1,232 @@
+from contextlib import ExitStack
+
+import concourse.mybir as mybir
+from concourse.masks import make_identity
+
+K, T, E, C, H, N = 512, 1024, 16, 128, 512, 512
+S = E * C
+FLOPS = 2 * 2 * K * H * T + 2 * H * N * S
+
+F32 = mybir.dt.float32
+BF16 = mybir.dt.bfloat16
+I32 = mybir.dt.int32
+U32 = mybir.dt.uint32
+U16 = mybir.dt.uint16
+U8 = mybir.dt.uint8
+FP8X4 = mybir.dt.float8_e4m3fn_x4
+FP4X4 = mybir.dt.float4_e2m1fn_x4
+MULT = mybir.AluOpType.mult
+MAX = mybir.AluOpType.max
+
+P = 128
+BANK = 512
+SLOT_GROUPS = (512, 512, 512, 256, 128, 128)
+TOKEN_CHUNKS = (384, 256, 128, 128, 128)
+
+
+def tile_moe_sup_glu_relu_kernel(
+    tc, x_words, x_scales, w1_words, w1_scales, w3_words, w3_scales, w2_words, w2_scales,
+    gate, offs, pos1, pos2, out_0, out_1, out_2,
+):
+    nc = tc.nc
+    with ExitStack() as ctx:
+        keep = ctx.enter_context(tc.tile_pool(name="keep", bufs=1))
+        ring = ctx.enter_context(tc.tile_pool(name="ring", bufs=2))
+        ring4 = ctx.enter_context(tc.tile_pool(name="ring4", bufs=4))
+        psum = ctx.enter_context(tc.psum_pool(name="psum", bufs=4))
+
+        def held(name, shape, dtype):
+            return keep.tile(shape, dtype, name=name, align_bytes=64)
+
+        def bank(tag):
+            return psum.tile([P, BANK], F32, name=tag)
+
+        def load_scale_rows(plane, rows, first):
+            for r in range(4):
+                dst = plane[first + r : P : 32, :].bitcast(I32)
+                src = rows[r]
+                if len(src.shape) == 3:
+                    dst = dst.rearrange("q (e n) -> q e n", e=src.shape[1])
+                nc.sync.dma_start(dst, src)
+
+        ws_raw = held("ws_raw", [P, H], U8)
+        xs = held("xs", [P, T], U8)
+        w2s = held("w2s", [P, E * N], U8)
+        nc.vector.memset(ws_raw[:].bitcast(I32), 0)
+        nc.vector.memset(xs[:].bitcast(I32), 0)
+        nc.vector.memset(w2s[:].bitcast(I32), 0)
+        ident = held("ident", [P, P], F32)
+        make_identity(nc, ident[:])
+
+        w3_raw = held("w3_raw", [P, H], I32)
+        w1_raw = held("w1_raw", [P, H], I32)
+        nc.sync.dma_start(w3_raw[:], w3_words[0].rearrange("p i d -> p (i d)").bitcast(I32))
+        nc.sync.dma_start(w1_raw[:], w1_words[0].rearrange("p i d -> p (i d)").bitcast(I32))
+        xw_dram = x_words[0].rearrange("p t d -> p (t d)").bitcast(I32)
+        xw = [held(f"xw{a}", [P, T // 2], I32) for a in range(2)]
+        nc.sync.dma_start(xw[0][:], xw_dram[:, : T // 2])
+        load_scale_rows(ws_raw, w3_scales[0].bitcast(I32).rearrange("(q r) n -> r q n", r=4), 0)
+        load_scale_rows(ws_raw, w1_scales[0].bitcast(I32).rearrange("(q r) n -> r q n", r=4), 4)
+        load_scale_rows(xs, x_scales[0].bitcast(I32).rearrange("(q r) n -> r q n", r=4), 0)
+        nc.sync.dma_start(xw[1][:], xw_dram[:, T // 2 :])
+        offs_t = held("offs_t", [P, S // 16], U16)
+        nc.sync.dma_start(offs_t[:], offs)
+        load_scale_rows(w2s, w2_scales.bitcast(I32).rearrange("e s (q r) n -> r q (e s) n", r=4), 0)
+        w2w = [held(f"w2w{a}", [P, 4 * 2 * N], U8) for a in range(4)]
+        for a in range(4):
+            nc.sync.dma_start(
+                w2w[a][:].bitcast(I32).rearrange("p (e c) -> p e c", e=4),
+                w2_words[4 * a : 4 * a + 4].bitcast(I32).rearrange("e s p c -> p (e s) c"),
+            )
+        pos_t = [held(f"pos{r}", [P, T // 16], U16) for r in range(2)]
+        nc.sync.dma_start(pos_t[0][:], pos1)
+        nc.sync.dma_start(pos_t[1][:], pos2)
+        gate_t = [held(f"gate{r}", [P, T], F32) for r in range(2)]
+        for r in range(2):
+            nc.sync.dma_start(gate_t[r][:], gate[r])
+
+        w3 = held("w3", [P, H], I32)
+        w1 = held("w1", [P, H], I32)
+        ws = held("ws", [P, H], U8)
+        for dst, src, run in ((w3, w3_raw, 4), (w1, w1_raw, 4), (ws, ws_raw, 16)):
+            nc.vector.tensor_copy(
+                dst[:].rearrange("p (t c i) -> p c t i", t=4, i=run),
+                src[:].rearrange("p (c i t) -> p c t i", t=4, i=run),
+            )
+
+        h = [held(f"h{u}", [P, 2 * T], BF16) for u in range(2)]
+        Q = BANK // 2
+
+        def first_product(w, first, u, tok, tag):
+            acc = bank(tag)
+            for e in range(2):
+                cols = slice(P * (2 * u + e), P * (2 * u + e + 1))
+                x0 = tok % (T // 2)
+                nc.tensor.matmul_mx(
+                    out=acc[:, Q * e : Q * (e + 1)],
+                    lhsT=w[:, cols].bitcast(FP8X4),
+                    lhsT_scale=ws[first:P, cols],
+                    rhs=xw[tok // (T // 2)][:, x0 : x0 + Q].bitcast(FP8X4),
+                    rhs_scale=xs[:, tok : tok + Q],
+                    start=True,
+                    stop=True,
+                )
+            return acc[:].rearrange("p (e t) -> p t e", e=2)
+
+        for half in range(2):
+            for u in range(2):
+                for tok in range(half * T // 2, (half + 1) * T // 2, Q):
+                    a3 = first_product(w3, 0, u, tok, "left")
+                    a1 = first_product(w1, 4, u, tok, "right")
+                    a3_sb = ring4.tile([P, Q, 2], F32, name="a3_sb")
+                    nc.scalar.copy(a3_sb[:], a3)
+                    nc.vector.scalar_tensor_tensor(
+                        out=h[u][:, 2 * tok : 2 * (tok + Q)].rearrange("p (t e) -> p t e", e=2),
+                        in0=a1, scalar=0.0, in1=a3_sb[:], op0=MAX, op1=MULT,
+                    )
+
+        starts = [sum(SLOT_GROUPS[:g]) for g in range(len(SLOT_GROUPS))]
+        last = len(SLOT_GROUPS) - 1
+        y = [held(f"y{j}", [P, S], F32) for j in range(4)]
+        woven = {}
+        codes = {}
+        planes = {}
+
+        def gather(g):
+            n, s0 = SLOT_GROUPS[g], starts[g]
+            lst = offs_t[:, s0 // 16 : (s0 + n) // 16]
+            woven[g] = ring.tile([P, 4 * n], BF16, name="woven", align_bytes=64)
+            words = woven[g][:].bitcast(U32).rearrange("p (s u) -> p s u", u=2)
+            if g == last:
+                for u in range(2):
+                    nc.vector.tensor_copy(words[:, :, u], h[u][:].bitcast(U32).indirect(lst))
+            else:
+                pairs = ring.tile([P, 2, n], U32, name="pairs")
+                for u in range(2):
+                    nc.vector.tensor_copy(pairs[:, u, :], h[u][:].bitcast(U32).indirect(lst))
+                nc.scalar.copy(words, pairs[:].rearrange("p u s -> p s u"))
+
+        def quantise(g):
+            n = SLOT_GROUPS[g]
+            codes[g] = held(f"codes{g}", [P, n], U32)
+            planes[g] = held(f"planes{g}", [P, n], U8)
+            nc.vector.quantize_mx(out=codes[g][:].bitcast(FP8X4), scales=planes[g][:], in_=woven[g][:])
+
+        def second_product(j, s0, n):
+            acc = bank("right")
+            for s in range(s0, s0 + n, C):
+                e = s // C
+                g = max(i for i in range(last + 1) if starts[i] <= s)
+                o = s - starts[g]
+                w0 = (e % 4) * 2 * N + 2 * P * j
+                nc.tensor.matmul_mx(
+                    out=acc[:, s - s0 : s - s0 + C],
+                    lhsT=w2w[e // 4][:, w0 : w0 + 2 * P].bitcast(FP4X4),
+                    lhsT_scale=w2s[:, e * N + P * j : e * N + P * (j + 1)],
+                    rhs=codes[g][:, o : o + C].bitcast(FP8X4),
+                    rhs_scale=planes[g][:, o : o + C],
+                    start=True,
+                    stop=True,
+                )
+            nc.scalar.copy(y[j][:, s0 : s0 + n], acc[:, :n])
+
+        early = {0: (1, 2), 1: (1,)}
+        gather(0)
+        for g in range(last + 1):
+            if g < last:
+                gather(g + 1)
+            quantise(g)
+            second_product(0, starts[g], SLOT_GROUPS[g])
+            for j in early.get(g, ()):
+                second_product(j, starts[g], SLOT_GROUPS[g])
+        for j in range(1, 4):
+            for b in range(S // BANK):
+                if j not in early.get(b, ()):
+                    second_product(j, b * BANK, BANK)
+
+        out_codes = held("out_codes", [P, T], U32)
+        out_plane = held("out_plane", [P, T], U8)
+        out_rows = out_0.rearrange("(p t) w -> p t w", t=4)
+        out_words = out_1[0].rearrange("p t d -> p (t d)").bitcast(I32)
+        tok = 0
+        for ci, n in enumerate(TOKEN_CHUNKS):
+            terms = [[held(f"term{ci}_{j}_{r}", [P, n], F32) for r in range(2)] for j in range(4)]
+            for j in range(4):
+                for r in range(2):
+                    nc.vector.tensor_tensor(
+                        terms[j][r][:],
+                        y[j][:].indirect(pos_t[r][:, tok // 16 : (tok + n) // 16]),
+                        gate_t[r][:, tok : tok + n],
+                        MULT,
+                    )
+            result = held(f"result{ci}", [P, 4, n], F32)
+            for b in range(0, n, P):
+                turned = bank("left")
+                for j in range(4):
+                    for r in range(2):
+                        nc.tensor.matmul(
+                            turned[:, P * j : P * (j + 1)], terms[j][r][:, b : b + P], ident[:],
+                            is_transpose=True, start=(r == 0), stop=(r == 1),
+                        )
+                dealt = ring4.tile([P, 4, P], F32, name="dealt")
+                nc.scalar.copy(dealt[:], turned[:].rearrange("p (m t) -> p t m", t=4))
+                back = bank("right")
+                for t in range(4):
+                    nc.tensor.transpose(back[:, P * t : P * (t + 1)], dealt[:, t, :], ident[:])
+                rounded = held(f"rounded{ci}_{b}", [P, 4 * P], BF16)
+                nc.scalar.copy(
+                    rounded[:].rearrange("p (w t) -> p w t", t=4),
+                    back[:].rearrange("p (t w) -> p w t", t=4),
+                )
+                nc.scalar.copy(result[:, :, b : b + P], back[:].rearrange("p (t w) -> p t w", t=4))
+                nc.vector.quantize_mx(
+                    out=out_codes[:, tok + b : tok + b + P].bitcast(FP8X4),
+                    scales=out_plane[:, tok + b : tok + b + P],
+                    in_=rounded[:],
+                )
+            nc.sync.dma_start(out_rows[:, :, tok : tok + n], result[:])
+            nc.sync.dma_start(out_words[:, tok : tok + n], out_codes[:, tok : tok + n].bitcast(I32))
+            tok = tok + n
+        scale_rows = out_2[0].bitcast(I32).rearrange("(q r) n -> r q n", r=4)
+        for r in range(4):
+            nc.scalar.dma_start(scale_rows[r], out_plane[r:P:32, :].bitcast(I32))

@@ -16,12 +16,12 @@ U8 = mybir.dt.uint8
 FP8X4 = mybir.dt.float8_e4m3fn_x4
 FP4X4 = mybir.dt.float4_e2m1fn_x4
 MULT = mybir.AluOpType.mult
+ADD = mybir.AluOpType.add
 MAX = mybir.AluOpType.max
 
 P = 128
 BANK = 512
-SLOT_GROUPS = (512, 512, 512, 256, 128, 128)
-TOKEN_CHUNKS = (384, 256, 128, 128, 128)
+SLOT_GROUPS = (256, 512, 512, 512, 128, 128)
 
 
 def tile_moe_sup_glu_relu_kernel(
@@ -34,6 +34,7 @@ def tile_moe_sup_glu_relu_kernel(
         ring = ctx.enter_context(tc.tile_pool(name="ring", bufs=2))
         ring4 = ctx.enter_context(tc.tile_pool(name="ring4", bufs=4))
         psum = ctx.enter_context(tc.psum_pool(name="psum", bufs=4))
+        left = ctx.enter_context(tc.psum_pool(name="left", bufs=1))
 
         def held(name, shape, dtype):
             return keep.tile(shape, dtype, name=name, align_bytes=64)
@@ -41,37 +42,39 @@ def tile_moe_sup_glu_relu_kernel(
         def bank(tag):
             return psum.tile([P, BANK], F32, name=tag)
 
-        def load_scale_rows(plane, rows, first):
+        def load_scale_rows(plane, rows, queues=(nc.sync,) * 4):
             for r in range(4):
-                dst = plane[first + r : P : 32, :].bitcast(I32)
+                dst = plane[r:P:32, :].bitcast(I32)
                 src = rows[r]
                 if len(src.shape) == 3:
                     dst = dst.rearrange("q (e n) -> q e n", e=src.shape[1])
-                nc.sync.dma_start(dst, src)
+                queues[r].dma_start(dst, src)
 
-        ws_raw = held("ws_raw", [P, H], U8)
+        w3s_raw = held("w3s_raw", [P, H], U8)
+        w1s_raw = held("w1s_raw", [P, H], U8)
         xs = held("xs", [P, T], U8)
         w2s = held("w2s", [P, E * N], U8)
-        nc.vector.memset(ws_raw[:].bitcast(I32), 0)
-        nc.vector.memset(xs[:].bitcast(I32), 0)
+        nc.gpsimd.memset(w3s_raw[:].bitcast(I32), 0)
+        nc.gpsimd.memset(xs[:].bitcast(I32), 0)
+        nc.vector.memset(w1s_raw[:].bitcast(I32), 0)
         nc.vector.memset(w2s[:].bitcast(I32), 0)
-        ident = held("ident", [P, P], F32)
-        make_identity(nc, ident[:])
 
         w3_raw = held("w3_raw", [P, H], I32)
         w1_raw = held("w1_raw", [P, H], I32)
-        nc.sync.dma_start(w3_raw[:], w3_words[0].rearrange("p i d -> p (i d)").bitcast(I32))
-        nc.sync.dma_start(w1_raw[:], w1_words[0].rearrange("p i d -> p (i d)").bitcast(I32))
         xw_dram = x_words[0].rearrange("p t d -> p (t d)").bitcast(I32)
         xw = [held(f"xw{a}", [P, T // 2], I32) for a in range(2)]
+        nc.sync.dma_start(w3_raw[:], w3_words[0].rearrange("p i d -> p (i d)").bitcast(I32))
         nc.sync.dma_start(xw[0][:], xw_dram[:, : T // 2])
-        load_scale_rows(ws_raw, w3_scales[0].bitcast(I32).rearrange("(q r) n -> r q n", r=4), 0)
-        load_scale_rows(ws_raw, w1_scales[0].bitcast(I32).rearrange("(q r) n -> r q n", r=4), 4)
-        load_scale_rows(xs, x_scales[0].bitcast(I32).rearrange("(q r) n -> r q n", r=4), 0)
+        load_scale_rows(w3s_raw, w3_scales[0].bitcast(I32).rearrange("(q r) n -> r q n", r=4))
+        load_scale_rows(xs, x_scales[0].bitcast(I32).rearrange("(q r) n -> r q n", r=4))
+        nc.sync.dma_start(w1_raw[:], w1_words[0].rearrange("p i d -> p (i d)").bitcast(I32))
+        load_scale_rows(w1s_raw, w1_scales[0].bitcast(I32).rearrange("(q r) n -> r q n", r=4))
         nc.sync.dma_start(xw[1][:], xw_dram[:, T // 2 :])
+        ident = held("ident", [P, P], F32)
+        make_identity(nc, ident[:])
         offs_t = held("offs_t", [P, S // 16], U16)
         nc.sync.dma_start(offs_t[:], offs)
-        load_scale_rows(w2s, w2_scales.bitcast(I32).rearrange("e s (q r) n -> r q (e s) n", r=4), 0)
+        load_scale_rows(w2s, w2_scales.bitcast(I32).rearrange("e s (q r) n -> r q (e s) n", r=4))
         w2w = [held(f"w2w{a}", [P, 4 * 2 * N], U8) for a in range(4)]
         for a in range(4):
             nc.sync.dma_start(
@@ -81,31 +84,33 @@ def tile_moe_sup_glu_relu_kernel(
         pos_t = [held(f"pos{r}", [P, T // 16], U16) for r in range(2)]
         nc.sync.dma_start(pos_t[0][:], pos1)
         nc.sync.dma_start(pos_t[1][:], pos2)
-        gate_t = [held(f"gate{r}", [P, T], F32) for r in range(2)]
+        gate_t = [held(f"gate{r}", [P, P + T], F32) for r in range(2)]
         for r in range(2):
-            nc.sync.dma_start(gate_t[r][:], gate[r])
+            nc.sync.dma_start(gate_t[r][:, P:], gate[r])
 
         w3 = held("w3", [P, H], I32)
         w1 = held("w1", [P, H], I32)
-        ws = held("ws", [P, H], U8)
-        for dst, src, run in ((w3, w3_raw, 4), (w1, w1_raw, 4), (ws, ws_raw, 16)):
-            nc.vector.tensor_copy(
-                dst[:].rearrange("p (t c i) -> p c t i", t=4, i=run),
-                src[:].rearrange("p (c i t) -> p c t i", t=4, i=run),
-            )
+        w3s = held("w3s", [P, H], U8)
+        w1s = held("w1s", [P, H], U8)
+        for pair in (((w3, w3_raw, 4), (w3s, w3s_raw, 16)), ((w1, w1_raw, 4), (w1s, w1s_raw, 16))):
+            for u in range(2):
+                for dst, src, run in pair:
+                    nc.vector.tensor_copy(
+                        dst[:].rearrange("p (t c i) -> p c t i", t=4, i=run)[:, :, 2 * u : 2 * u + 2, :],
+                        src[:].rearrange("p (c i t) -> p c t i", t=4, i=run)[:, :, 2 * u : 2 * u + 2, :],
+                    )
 
         h = [held(f"h{u}", [P, 2 * T], BF16) for u in range(2)]
         Q = BANK // 2
 
-        def first_product(w, first, u, tok, tag):
-            acc = bank(tag)
+        def first_product(w, ws, u, tok, acc):
             for e in range(2):
                 cols = slice(P * (2 * u + e), P * (2 * u + e + 1))
                 x0 = tok % (T // 2)
                 nc.tensor.matmul_mx(
                     out=acc[:, Q * e : Q * (e + 1)],
                     lhsT=w[:, cols].bitcast(FP8X4),
-                    lhsT_scale=ws[first:P, cols],
+                    lhsT_scale=ws[:, cols],
                     rhs=xw[tok // (T // 2)][:, x0 : x0 + Q].bitcast(FP8X4),
                     rhs_scale=xs[:, tok : tok + Q],
                     start=True,
@@ -113,17 +118,22 @@ def tile_moe_sup_glu_relu_kernel(
                 )
             return acc[:].rearrange("p (e t) -> p t e", e=2)
 
-        for half in range(2):
-            for u in range(2):
-                for tok in range(half * T // 2, (half + 1) * T // 2, Q):
-                    a3 = first_product(w3, 0, u, tok, "left")
-                    a1 = first_product(w1, 4, u, tok, "right")
-                    a3_sb = ring4.tile([P, Q, 2], F32, name="a3_sb")
-                    nc.scalar.copy(a3_sb[:], a3)
-                    nc.vector.scalar_tensor_tensor(
-                        out=h[u][:, 2 * tok : 2 * (tok + Q)].rearrange("p (t e) -> p t e", e=2),
-                        in0=a1, scalar=0.0, in1=a3_sb[:], op0=MAX, op1=MULT,
-                    )
+        steps = [
+            (u, tok) for half in range(2) for u in range(2)
+            for tok in range(half * T // 2, (half + 1) * T // 2, Q)
+        ]
+        ahead = 3
+        a3_sb = [held(f"a3_sb{i}", [P, Q, 2], F32) for i in range(len(steps))]
+        for i in range(len(steps) + ahead):
+            if i >= ahead:
+                u, tok = steps[i - ahead]
+                nc.vector.scalar_tensor_tensor(
+                    out=h[u][:, 2 * tok : 2 * (tok + Q)].rearrange("p (t e) -> p t e", e=2),
+                    in0=first_product(w1, w1s, u, tok, bank("right")),
+                    scalar=0.0, in1=a3_sb[i - ahead][:], op0=MAX, op1=MULT,
+                )
+            if i < len(steps):
+                nc.scalar.copy(a3_sb[i][:], first_product(w3, w3s, *steps[i], left.tile([P, BANK], F32, name=f"left{i % 4}")))
 
         starts = [sum(SLOT_GROUPS[:g]) for g in range(len(SLOT_GROUPS))]
         last = len(SLOT_GROUPS) - 1
@@ -170,7 +180,7 @@ def tile_moe_sup_glu_relu_kernel(
                 )
             nc.scalar.copy(y[j][:, s0 : s0 + n], acc[:, :n])
 
-        early = {0: (1, 2), 1: (1,)}
+        early = {0: (1, 2, 3), 1: (1,)}
         gather(0)
         for g in range(last + 1):
             if g < last:
@@ -180,53 +190,108 @@ def tile_moe_sup_glu_relu_kernel(
             for j in early.get(g, ()):
                 second_product(j, starts[g], SLOT_GROUPS[g])
         for j in range(1, 4):
-            for b in range(S // BANK):
-                if j not in early.get(b, ()):
-                    second_product(j, b * BANK, BANK)
+            first = min(starts[g] for g in range(last + 1) if j not in early.get(g, ()))
+            for s0 in range(first, S, BANK):
+                second_product(j, s0, min(BANK, S - s0))
 
         out_codes = held("out_codes", [P, T], U32)
         out_plane = held("out_plane", [P, T], U8)
         out_rows = out_0.rearrange("(p t) w -> p t w", t=4)
         out_words = out_1[0].rearrange("p t d -> p (t d)").bitcast(I32)
-        tok = 0
-        for ci, n in enumerate(TOKEN_CHUNKS):
-            terms = [[held(f"term{ci}_{j}_{r}", [P, n], F32) for r in range(2)] for j in range(4)]
+        blocks = T // P
+        head = 3
+        backs = {}
+
+        def combine(b, n):
+            tok = b * P
+            if b == 0:
+                terms = [[held(f"term{j}_{r}", [P, n], F32)[:] for r in range(2)] for j in range(4)]
+            else:
+                terms = [[gate_t[r][:, tok - P * j : tok - P * j + P] for r in range(2)] for j in range(4)]
             for j in range(4):
                 for r in range(2):
                     nc.vector.tensor_tensor(
-                        terms[j][r][:],
+                        terms[j][r],
                         y[j][:].indirect(pos_t[r][:, tok // 16 : (tok + n) // 16]),
-                        gate_t[r][:, tok : tok + n],
+                        gate_t[r][:, P + tok : P + tok + n],
                         MULT,
                     )
-            result = held(f"result{ci}", [P, 4, n], F32)
-            for b in range(0, n, P):
-                turned = bank("left")
-                for j in range(4):
+            return terms
+
+        def turn(b, terms, o):
+            dealt = ring4.tile([P, 4, P], F32, name="dealt")
+            for rows in ((0, 4),) if b < head else ((0, 2), (2, 4)):
+                turned = left.tile([P, BANK], F32, name=f"left{b if b < head else 1 + rows[0] // 2}")
+                for j in range(*rows):
                     for r in range(2):
                         nc.tensor.matmul(
-                            turned[:, P * j : P * (j + 1)], terms[j][r][:, b : b + P], ident[:],
+                            turned[:, P * j : P * (j + 1)], terms[j][r][:, o : o + P], ident[:],
                             is_transpose=True, start=(r == 0), stop=(r == 1),
                         )
-                dealt = ring4.tile([P, 4, P], F32, name="dealt")
-                nc.scalar.copy(dealt[:], turned[:].rearrange("p (m t) -> p t m", t=4))
-                back = bank("right")
-                for t in range(4):
-                    nc.tensor.transpose(back[:, P * t : P * (t + 1)], dealt[:, t, :], ident[:])
-                rounded = held(f"rounded{ci}_{b}", [P, 4 * P], BF16)
                 nc.scalar.copy(
-                    rounded[:].rearrange("p (w t) -> p w t", t=4),
-                    back[:].rearrange("p (t w) -> p w t", t=4),
+                    dealt[:, :, 32 * rows[0] : 32 * rows[1]],
+                    turned[:, P * rows[0] : P * rows[1]].rearrange("p (m t) -> p t m", t=4),
                 )
-                nc.scalar.copy(result[:, :, b : b + P], back[:].rearrange("p (t w) -> p t w", t=4))
-                nc.vector.quantize_mx(
-                    out=out_codes[:, tok + b : tok + b + P].bitcast(FP8X4),
-                    scales=out_plane[:, tok + b : tok + b + P],
-                    in_=rounded[:],
+            backs[b] = bank("right")
+            for t in range(4):
+                nc.tensor.transpose(backs[b][:, P * t : P * (t + 1)], dealt[:, t, :], ident[:])
+
+        def finish(b):
+            cols = slice(b * P, (b + 1) * P)
+            rounded = held(f"rounded{b}", [P, 4 * P], BF16)
+            nc.scalar.copy(
+                rounded[:].rearrange("p (w t) -> p w t", t=4),
+                backs[b][:].rearrange("p (t w) -> p w t", t=4),
+            )
+            result = held(f"result{b}", [P, 4, P], F32)
+            nc.scalar.copy(result[:], backs[b][:].rearrange("p (t w) -> p t w", t=4))
+            nc.vector.quantize_mx(out=out_codes[:, cols].bitcast(FP8X4), scales=out_plane[:, cols], in_=rounded[:])
+            nc.sync.dma_start(out_rows[:, :, cols], result[:])
+            if b == blocks - 2:
+                nc.sync.dma_start(out_words[:, : T - P], out_codes[:, : T - P].bitcast(I32))
+
+        def finish_last(b, terms):
+            tok = b * P
+            cols = slice(tok, T)
+            dealt = held("dealt_pairs", [P, 2, P, 2], BF16)
+            for rows in ((0, 3), (3, 4)):
+                turned = left.tile([P, BANK], F32, name=f"left{1 + rows[0] // 2}")
+                for j in range(*rows):
+                    for r in range(2):
+                        nc.tensor.matmul(
+                            turned[:, P * j : P * (j + 1)], terms[j][r], ident[:],
+                            is_transpose=True, start=(r == 0), stop=(r == 1),
+                        )
+                nc.scalar.copy(
+                    dealt[:, :, 32 * rows[0] : 32 * rows[1], :],
+                    turned[:, P * rows[0] : P * rows[1]].rearrange("p (m u e) -> p u m e", u=2, e=2),
                 )
-            nc.sync.dma_start(out_rows[:, :, tok : tok + n], result[:])
-            nc.sync.dma_start(out_words[:, tok : tok + n], out_codes[:, tok : tok + n].bitcast(I32))
-            tok = tok + n
+            words = dealt[:].rearrange("p u m e -> p (u m e)").bitcast(F32)
+            back = bank("right")
+            for u in range(2):
+                nc.tensor.transpose(back[:, P * u : P * (u + 1)], words[:, P * u : P * (u + 1)], ident[:])
+            finish(b - 1)
+            result = held("result_last", [P, 4, P], F32)
+            spent = slice(tok - 3 * P, tok + P)
+            both = [g[:, spent].rearrange("p (j w) -> p j w", j=4)[:, ::-1, :] for g in gate_t]
+            nc.vector.tensor_tensor(result[:], both[0], both[1], ADD)
+            nc.sync.dma_start(out_0.rearrange("(j p) w -> p j w", j=4)[:, :, cols], result[:])
+            rounded = held("rounded_last", [P, 4 * P], BF16)
+            nc.scalar.copy(
+                rounded[:].bitcast(F32).rearrange("p (w u) -> p w u", u=2),
+                back[:, : 2 * P].rearrange("p (u w) -> p w u", u=2),
+            )
+            nc.vector.quantize_mx(out=out_codes[:, cols].bitcast(FP8X4), scales=out_plane[:, cols], in_=rounded[:])
+            nc.sync.dma_start(out_words[:, cols], out_codes[:, cols].bitcast(I32))
+
+        terms = combine(0, head * P)
+        for b in range(blocks - 1):
+            if b >= head:
+                terms = combine(b, P)
+            turn(b, terms, b * P if b < head else 0)
+            if b:
+                finish(b - 1)
+        finish_last(blocks - 1, combine(blocks - 1, P))
         scale_rows = out_2[0].bitcast(I32).rearrange("(q r) n -> r q n", r=4)
         for r in range(4):
             nc.scalar.dma_start(scale_rows[r], out_plane[r:P:32, :].bitcast(I32))

@@ -17,11 +17,12 @@ FP8X4 = mybir.dt.float8_e4m3fn_x4
 FP4X4 = mybir.dt.float4_e2m1fn_x4
 MULT = mybir.AluOpType.mult
 ADD = mybir.AluOpType.add
+RELU = mybir.ActivationFunctionType.Relu
 MAX = mybir.AluOpType.max
 
 P = 128
 BANK = 512
-SLOT_GROUPS = (256, 512, 512, 512, 128, 128)
+SLOT_GROUPS = (256, 512, 512, 512, 256)
 
 
 def tile_moe_sup_glu_relu_kernel(
@@ -56,8 +57,8 @@ def tile_moe_sup_glu_relu_kernel(
         w2s = held("w2s", [P, E * N], U8)
         nc.gpsimd.memset(w3s_raw[:].bitcast(I32), 0)
         nc.gpsimd.memset(xs[:].bitcast(I32), 0)
-        nc.vector.memset(w1s_raw[:].bitcast(I32), 0)
-        nc.vector.memset(w2s[:].bitcast(I32), 0)
+        nc.gpsimd.memset(w1s_raw[:].bitcast(I32), 0)
+        nc.gpsimd.memset(w2s[:].bitcast(I32), 0)
 
         w3_raw = held("w3_raw", [P, H], I32)
         w1_raw = held("w1_raw", [P, H], I32)
@@ -84,9 +85,9 @@ def tile_moe_sup_glu_relu_kernel(
         pos_t = [held(f"pos{r}", [P, T // 16], U16) for r in range(2)]
         nc.sync.dma_start(pos_t[0][:], pos1)
         nc.sync.dma_start(pos_t[1][:], pos2)
-        gate_t = [held(f"gate{r}", [P, P + T], F32) for r in range(2)]
+        gate_t = [held(f"gate{r}", [P, 4 * P + T], F32) for r in range(2)]
         for r in range(2):
-            nc.sync.dma_start(gate_t[r][:, P:], gate[r])
+            nc.sync.dma_start(gate_t[r][:, 4 * P :], gate[r])
 
         w3 = held("w3", [P, H], I32)
         w1 = held("w1", [P, H], I32)
@@ -127,11 +128,16 @@ def tile_moe_sup_glu_relu_kernel(
         for i in range(len(steps) + ahead):
             if i >= ahead:
                 u, tok = steps[i - ahead]
-                nc.vector.scalar_tensor_tensor(
-                    out=h[u][:, 2 * tok : 2 * (tok + Q)].rearrange("p (t e) -> p t e", e=2),
-                    in0=first_product(w1, w1s, u, tok, bank("right")),
-                    scalar=0.0, in1=a3_sb[i - ahead][:], op0=MAX, op1=MULT,
-                )
+                a1 = first_product(w1, w1s, u, tok, bank("right"))
+                out = h[u][:, 2 * tok : 2 * (tok + Q)].rearrange("p (t e) -> p t e", e=2)
+                if i - ahead in (0, 2):
+                    a1_sb = held(f"a1_sb{i}", [P, Q, 2], F32)
+                    nc.scalar.activation(a1_sb[:], a1, RELU)
+                    nc.gpsimd.tensor_tensor(out, a1_sb[:], a3_sb[i - ahead][:], MULT)
+                else:
+                    nc.vector.scalar_tensor_tensor(
+                        out=out, in0=a1, scalar=0.0, in1=a3_sb[i - ahead][:], op0=MAX, op1=MULT,
+                    )
             if i < len(steps):
                 nc.scalar.copy(a3_sb[i][:], first_product(w3, w3s, *steps[i], left.tile([P, BANK], F32, name=f"left{i % 4}")))
 
@@ -181,14 +187,18 @@ def tile_moe_sup_glu_relu_kernel(
             nc.scalar.copy(y[j][:, s0 : s0 + n], acc[:, :n])
 
         early = {0: (1, 2, 3), 1: (1,)}
+        def products(g):
+            for j in (0, *early.get(g, ())):
+                second_product(j, starts[g], SLOT_GROUPS[g])
+
         gather(0)
         for g in range(last + 1):
             if g < last:
                 gather(g + 1)
             quantise(g)
-            second_product(0, starts[g], SLOT_GROUPS[g])
-            for j in early.get(g, ()):
-                second_product(j, starts[g], SLOT_GROUPS[g])
+            if g:
+                products(g - 1)
+        products(last)
         for j in range(1, 4):
             first = min(starts[g] for g in range(last + 1) if j not in early.get(g, ()))
             for s0 in range(first, S, BANK):
@@ -205,15 +215,17 @@ def tile_moe_sup_glu_relu_kernel(
         def combine(b, n):
             tok = b * P
             if b == 0:
-                terms = [[held(f"term{j}_{r}", [P, n], F32)[:] for r in range(2)] for j in range(4)]
+                terms = [[held(f"term{j}_{r}", [P, n], F32)[:] for r in range(2)] for j in range(3)]
+                terms.append([g[:, :n] for g in gate_t])
             else:
-                terms = [[gate_t[r][:, tok - P * j : tok - P * j + P] for r in range(2)] for j in range(4)]
+                places = [3 + b] + [3 * (b % 2) + j % 3 for j in range(1, 4)]
+                terms = [[g[:, P * place : P * (place + 1)] for g in gate_t] for place in places]
             for j in range(4):
                 for r in range(2):
                     nc.vector.tensor_tensor(
                         terms[j][r],
                         y[j][:].indirect(pos_t[r][:, tok // 16 : (tok + n) // 16]),
-                        gate_t[r][:, P + tok : P + tok + n],
+                        gate_t[r][:, 4 * P + tok : 4 * P + tok + n],
                         MULT,
                     )
             return terms
@@ -272,9 +284,8 @@ def tile_moe_sup_glu_relu_kernel(
                 nc.tensor.transpose(back[:, P * u : P * (u + 1)], words[:, P * u : P * (u + 1)], ident[:])
             finish(b - 1)
             result = held("result_last", [P, 4, P], F32)
-            spent = slice(tok - 3 * P, tok + P)
-            both = [g[:, spent].rearrange("p (j w) -> p j w", j=4)[:, ::-1, :] for g in gate_t]
-            nc.vector.tensor_tensor(result[:], both[0], both[1], ADD)
+            for j in range(4):
+                nc.vector.tensor_tensor(result[:, j, :], terms[j][0], terms[j][1], ADD)
             nc.sync.dma_start(out_0.rearrange("(j p) w -> p j w", j=4)[:, :, cols], result[:])
             rounded = held("rounded_last", [P, 4 * P], BF16)
             nc.scalar.copy(

@@ -89,6 +89,12 @@ def tile_moe_sup_glu_relu_kernel(
         for r in range(2):
             nc.sync.dma_start(gate_t[r][:, 4 * P :], gate[r])
 
+        warm = bank("right")
+        for i in range(3):
+            nc.tensor.matmul_mx(
+                out=warm[:], lhsT=w3_raw[:, :P].bitcast(FP8X4), lhsT_scale=w3s_raw[:, :P],
+                rhs=w3_raw[:].bitcast(FP8X4), rhs_scale=w3s_raw[:], start=(i == 0), stop=(i == 2),
+            )
         w3 = held("w3", [P, H], I32)
         w1 = held("w1", [P, H], I32)
         w3s = held("w3s", [P, H], U8)

@@ -22,7 +22,9 @@ MAX = mybir.AluOpType.max
 
 P = 128
 BANK = 512
-SLOT_GROUPS = (256, 512, 512, 512, 256)
+CHUNK = 256
+LAG = 3
+GPSIMD_STEPS = (4, 5, 6)
 
 
 def tile_moe_sup_glu_relu_kernel(
@@ -32,24 +34,22 @@ def tile_moe_sup_glu_relu_kernel(
     nc = tc.nc
     with ExitStack() as ctx:
         keep = ctx.enter_context(tc.tile_pool(name="keep", bufs=1))
-        ring = ctx.enter_context(tc.tile_pool(name="ring", bufs=2))
         ring4 = ctx.enter_context(tc.tile_pool(name="ring4", bufs=4))
-        psum = ctx.enter_context(tc.psum_pool(name="psum", bufs=4))
-        left = ctx.enter_context(tc.psum_pool(name="left", bufs=1))
+        psum = ctx.enter_context(tc.psum_pool(name="psum", bufs=1))
 
-        def held(name, shape, dtype):
-            return keep.tile(shape, dtype, name=name, align_bytes=64)
+        def held(name, shape, dtype, tag=""):
+            return keep.tile(shape, dtype, name=name, tag=tag or name, align_bytes=64)
 
-        def bank(tag):
-            return psum.tile([P, BANK], F32, name=tag)
+        def bank(i):
+            return psum.tile([P, BANK], F32, name=f"bank{i}")
 
-        def load_scale_rows(plane, rows, queues=(nc.sync,) * 4):
-            for r in range(4):
+        def load_scale_rows(plane, rows, which=range(4), queue=nc.sync):
+            for r in which:
                 dst = plane[r:P:32, :].bitcast(I32)
                 src = rows[r]
                 if len(src.shape) == 3:
                     dst = dst.rearrange("q (e n) -> q e n", e=src.shape[1])
-                queues[r].dma_start(dst, src)
+                queue.dma_start(dst, src)
 
         w3s_raw = held("w3s_raw", [P, H], U8)
         w1s_raw = held("w1s_raw", [P, H], U8)
@@ -57,31 +57,32 @@ def tile_moe_sup_glu_relu_kernel(
         w2s = held("w2s", [P, E * N], U8)
         nc.gpsimd.memset(w3s_raw[:].bitcast(I32), 0)
         nc.gpsimd.memset(xs[:].bitcast(I32), 0)
-        nc.gpsimd.memset(w1s_raw[:].bitcast(I32), 0)
-        nc.gpsimd.memset(w2s[:].bitcast(I32), 0)
+        nc.vector.memset(w1s_raw[:].bitcast(I32), 0)
+        nc.vector.memset(w2s[:].bitcast(I32), 0)
 
         w3_raw = held("w3_raw", [P, H], I32)
         w1_raw = held("w1_raw", [P, H], I32)
         xw_dram = x_words[0].rearrange("p t d -> p (t d)").bitcast(I32)
-        xw = [held(f"xw{a}", [P, T // 2], I32) for a in range(2)]
+        xw = held("xw", [P, T], I32)
+        xs_rows = x_scales[0].bitcast(I32).rearrange("(q r) n -> r q n", r=4)
+        w1s_rows = w1_scales[0].bitcast(I32).rearrange("(q r) n -> r q n", r=4)
+        load_scale_rows(xs, xs_rows, (3,), nc.gpsimd)
         nc.sync.dma_start(w3_raw[:], w3_words[0].rearrange("p i d -> p (i d)").bitcast(I32))
-        nc.sync.dma_start(xw[0][:], xw_dram[:, : T // 2])
         load_scale_rows(w3s_raw, w3_scales[0].bitcast(I32).rearrange("(q r) n -> r q n", r=4))
-        load_scale_rows(xs, x_scales[0].bitcast(I32).rearrange("(q r) n -> r q n", r=4))
+        load_scale_rows(xs, xs_rows, (0, 1))
+        nc.sync.dma_start(xw[:], xw_dram)
+        load_scale_rows(xs, xs_rows, (2,))
         nc.sync.dma_start(w1_raw[:], w1_words[0].rearrange("p i d -> p (i d)").bitcast(I32))
-        load_scale_rows(w1s_raw, w1_scales[0].bitcast(I32).rearrange("(q r) n -> r q n", r=4))
-        nc.sync.dma_start(xw[1][:], xw_dram[:, T // 2 :])
-        ident = held("ident", [P, P], F32)
-        make_identity(nc, ident[:])
+        load_scale_rows(w1s_raw, w1s_rows)
         offs_t = held("offs_t", [P, S // 16], U16)
         nc.sync.dma_start(offs_t[:], offs)
-        load_scale_rows(w2s, w2_scales.bitcast(I32).rearrange("e s (q r) n -> r q (e s) n", r=4))
         w2w = [held(f"w2w{a}", [P, 4 * 2 * N], U8) for a in range(4)]
-        for a in range(4):
+        for a in reversed(range(4)):
             nc.sync.dma_start(
                 w2w[a][:].bitcast(I32).rearrange("p (e c) -> p e c", e=4),
                 w2_words[4 * a : 4 * a + 4].bitcast(I32).rearrange("e s p c -> p (e s) c"),
             )
+        load_scale_rows(w2s, w2_scales.bitcast(I32).rearrange("e s (q r) n -> r q (e s) n", r=4))
         pos_t = [held(f"pos{r}", [P, T // 16], U16) for r in range(2)]
         nc.sync.dma_start(pos_t[0][:], pos1)
         nc.sync.dma_start(pos_t[1][:], pos2)
@@ -89,7 +90,7 @@ def tile_moe_sup_glu_relu_kernel(
         for r in range(2):
             nc.sync.dma_start(gate_t[r][:, 4 * P :], gate[r])
 
-        warm = bank("right")
+        warm = bank(7)
         for i in range(3):
             nc.tensor.matmul_mx(
                 out=warm[:], lhsT=w3_raw[:, :P].bitcast(FP8X4), lhsT_scale=w3s_raw[:, :P],
@@ -107,18 +108,19 @@ def tile_moe_sup_glu_relu_kernel(
                         src[:].rearrange("p (c i t) -> p c t i", t=4, i=run)[:, :, 2 * u : 2 * u + 2, :],
                     )
 
+        ident = held("ident", [P, P], F32, tag="w3_raw")
+        make_identity(nc, ident[:])
         h = [held(f"h{u}", [P, 2 * T], BF16) for u in range(2)]
         Q = BANK // 2
 
         def first_product(w, ws, u, tok, acc):
             for e in range(2):
                 cols = slice(P * (2 * u + e), P * (2 * u + e + 1))
-                x0 = tok % (T // 2)
                 nc.tensor.matmul_mx(
                     out=acc[:, Q * e : Q * (e + 1)],
                     lhsT=w[:, cols].bitcast(FP8X4),
                     lhsT_scale=ws[:, cols],
-                    rhs=xw[tok // (T // 2)][:, x0 : x0 + Q].bitcast(FP8X4),
+                    rhs=xw[:, tok : tok + Q].bitcast(FP8X4),
                     rhs_scale=xs[:, tok : tok + Q],
                     start=True,
                     stop=True,
@@ -126,60 +128,70 @@ def tile_moe_sup_glu_relu_kernel(
             return acc[:].rearrange("p (e t) -> p t e", e=2)
 
         steps = [
-            (u, tok) for half in range(2) for u in range(2)
-            for tok in range(half * T // 2, (half + 1) * T // 2, Q)
+            (u, tok) for u in range(2) for tok in range(0, T, Q)
         ]
-        ahead = 3
         a3_sb = [held(f"a3_sb{i}", [P, Q, 2], F32) for i in range(len(steps))]
-        for i in range(len(steps) + ahead):
-            if i >= ahead:
-                u, tok = steps[i - ahead]
-                a1 = first_product(w1, w1s, u, tok, bank("right"))
-                out = h[u][:, 2 * tok : 2 * (tok + Q)].rearrange("p (t e) -> p t e", e=2)
-                if i - ahead in (0, 2):
-                    a1_sb = held(f"a1_sb{i}", [P, Q, 2], F32)
-                    nc.scalar.activation(a1_sb[:], a1, RELU)
-                    nc.gpsimd.tensor_tensor(out, a1_sb[:], a3_sb[i - ahead][:], MULT)
-                else:
-                    nc.vector.scalar_tensor_tensor(
-                        out=out, in0=a1, scalar=0.0, in1=a3_sb[i - ahead][:], op0=MAX, op1=MULT,
-                    )
-            if i < len(steps):
-                nc.scalar.copy(a3_sb[i][:], first_product(w3, w3s, *steps[i], left.tile([P, BANK], F32, name=f"left{i % 4}")))
 
-        starts = [sum(SLOT_GROUPS[:g]) for g in range(len(SLOT_GROUPS))]
-        last = len(SLOT_GROUPS) - 1
+        def linear_half(i):
+            nc.scalar.copy(a3_sb[i][:], first_product(w3, w3s, *steps[i], bank(i % 4)))
+
+        def gated_half(i):
+            u, tok = steps[i]
+            a1 = first_product(w1, w1s, u, tok, bank(4 + i % 4))
+            out = h[u][:, 2 * tok : 2 * (tok + Q)].rearrange("p (t e) -> p t e", e=2)
+            if i in GPSIMD_STEPS:
+                a1_sb = held(f"a1_sb{i}", [P, Q, 2], F32)
+                nc.scalar.activation(a1_sb[:], a1, RELU)
+                nc.gpsimd.tensor_tensor(out, a1_sb[:], a3_sb[i][:], MULT)
+            else:
+                nc.vector.scalar_tensor_tensor(
+                    out=out, in0=a1, scalar=0.0, in1=a3_sb[i][:], op0=MAX, op1=MULT,
+                )
+
+        for i in range(4):
+            linear_half(i)
+        for i in range(4):
+            gated_half(i)
+        for i in range(4, 8):
+            linear_half(i)
+            gated_half(i)
+
+        chunks = S // CHUNK
         y = [held(f"y{j}", [P, S], F32) for j in range(4)]
         woven = {}
         codes = {}
         planes = {}
+        pairs = held("pairs", [P, (chunks + LAG) * CHUNK], U32)
+        rows = pairs[:].rearrange("p (r s) -> p r s", s=CHUNK)
 
-        def gather(g):
-            n, s0 = SLOT_GROUPS[g], starts[g]
-            lst = offs_t[:, s0 // 16 : (s0 + n) // 16]
-            woven[g] = ring.tile([P, 4 * n], BF16, name="woven", align_bytes=64)
-            words = woven[g][:].bitcast(U32).rearrange("p (s u) -> p s u", u=2)
-            if g == last:
+        def slots(s0, n):
+            return offs_t[:, s0 // 16 : (s0 + n) // 16]
+
+        def gather(c):
+            lst = slots(c * CHUNK, CHUNK)
+            if c == 0:
+                both = pairs[:, (2 + LAG) * CHUNK : (4 + LAG) * CHUNK]
+                woven[c] = both.bitcast(BF16)
                 for u in range(2):
-                    nc.vector.tensor_copy(words[:, :, u], h[u][:].bitcast(U32).indirect(lst))
+                    nc.vector.tensor_copy(both.rearrange("p (s u) -> p s u", u=2)[:, :, u], h[u][:].bitcast(U32).indirect(lst))
             else:
-                pairs = ring.tile([P, 2, n], U32, name="pairs")
-                for u in range(2):
-                    nc.vector.tensor_copy(pairs[:, u, :], h[u][:].bitcast(U32).indirect(lst))
-                nc.scalar.copy(words, pairs[:].rearrange("p u s -> p s u"))
+                woven[c] = held(f"woven{c}", [P, 4 * CHUNK], BF16)[:]
+                nc.vector.tensor_copy(rows[:, c + LAG, :], h[1][:].bitcast(U32).indirect(lst))
+                nc.scalar.copy(
+                    woven[c].bitcast(U32).rearrange("p (s u) -> p s u", u=2),
+                    rows[:, c : c + LAG + 1 : LAG, :].rearrange("p u s -> p s u"),
+                )
 
-        def quantise(g):
-            n = SLOT_GROUPS[g]
-            codes[g] = held(f"codes{g}", [P, n], U32)
-            planes[g] = held(f"planes{g}", [P, n], U8)
-            nc.vector.quantize_mx(out=codes[g][:].bitcast(FP8X4), scales=planes[g][:], in_=woven[g][:])
+        def quantise(c):
+            codes[c] = held(f"codes{c}", [P, CHUNK], U32)
+            planes[c] = held(f"planes{c}", [P, CHUNK], U8)
+            nc.vector.quantize_mx(out=codes[c][:].bitcast(FP8X4), scales=planes[c][:], in_=woven[c])
 
-        def second_product(j, s0, n):
-            acc = bank("right")
+        def second_product(j, s0, n, b):
+            acc = bank(b)
             for s in range(s0, s0 + n, C):
                 e = s // C
-                g = max(i for i in range(last + 1) if starts[i] <= s)
-                o = s - starts[g]
+                g, o = divmod(s, CHUNK)
                 w0 = (e % 4) * 2 * N + 2 * P * j
                 nc.tensor.matmul_mx(
                     out=acc[:, s - s0 : s - s0 + C],
@@ -190,28 +202,30 @@ def tile_moe_sup_glu_relu_kernel(
                     start=True,
                     stop=True,
                 )
-            nc.scalar.copy(y[j][:, s0 : s0 + n], acc[:, :n])
+            return y[j][:, s0 : s0 + n], acc[:, :n]
 
-        early = {0: (1, 2, 3), 1: (1,)}
-        def products(g):
-            for j in (0, *early.get(g, ())):
-                second_product(j, starts[g], SLOT_GROUPS[g])
-
+        for s0, n in ((5 * CHUNK, 3 * CHUNK), (3 * CHUNK, 2 * CHUNK), (CHUNK, 2 * CHUNK)):
+            nc.vector.tensor_copy(pairs[:, s0 : s0 + n], h[0][:].bitcast(U32).indirect(slots(s0, n)))
+        for c in range(chunks - 1, 0, -1):
+            gather(c)
+            if c + 2 < chunks:
+                quantise(c + 2)
+        quantise(2)
         gather(0)
-        for g in range(last + 1):
-            if g < last:
-                gather(g + 1)
-            quantise(g)
-            if g:
-                products(g - 1)
-        products(last)
-        for j in range(1, 4):
-            first = min(starts[g] for g in range(last + 1) if j not in early.get(g, ()))
-            for s0 in range(first, S, BANK):
-                second_product(j, s0, min(BANK, S - s0))
+        for q in (3, 2, 1):
+            nc.scalar.copy(*second_product(0, q * BANK, BANK, 7 - q))
+        by_vector = [second_product(1, q * BANK, BANK, 3 - q) for q in (3, 2)]
+        quantise(1)
+        quantise(0)
+        nc.scalar.copy(*second_product(0, CHUNK, CHUNK, 7))
+        nc.scalar.copy(*second_product(0, 0, CHUNK, 2))
+        for pair in by_vector:
+            nc.vector.tensor_copy(*pair)
+        rest = [(1, 1), (1, 0)] + [(j, q) for j in (2, 3) for q in (3, 2, 1, 0)]
+        for (j, q), b in zip(rest, (3, 4, 5, 6, 7, 2, 3, 4, 0, 1)):
+            nc.scalar.copy(*second_product(j, q * BANK, BANK, b))
 
-        out_codes = held("out_codes", [P, T], U32)
-        out_plane = held("out_plane", [P, T], U8)
+        rounded = held("rounded", [P, 4 * T], BF16)
         out_rows = out_0.rearrange("(p t) w -> p t w", t=4)
         out_words = out_1[0].rearrange("p t d -> p (t d)").bitcast(I32)
         blocks = T // P
@@ -224,91 +238,113 @@ def tile_moe_sup_glu_relu_kernel(
                 terms = [[held(f"term{j}_{r}", [P, n], F32)[:] for r in range(2)] for j in range(3)]
                 terms.append([g[:, :n] for g in gate_t])
             else:
-                places = [3 + b] + [3 * (b % 2) + j % 3 for j in range(1, 4)]
+                places = [4 * (b % 2) + j for j in range(3)] + [3 if b in (3, 5) else 7]
                 terms = [[g[:, P * place : P * (place + 1)] for g in gate_t] for place in places]
             for j in range(4):
-                for r in range(2):
-                    nc.vector.tensor_tensor(
-                        terms[j][r],
-                        y[j][:].indirect(pos_t[r][:, tok // 16 : (tok + n) // 16]),
-                        gate_t[r][:, 4 * P + tok : 4 * P + tok + n],
-                        MULT,
-                    )
+                width = P if j == 3 else n
+                for o in range(0, n, width):
+                    for r in range(2):
+                        nc.vector.tensor_tensor(
+                            terms[j][r][:, o : o + width],
+                            y[j][:].indirect(pos_t[r][:, (tok + o) // 16 : (tok + o + width) // 16]),
+                            gate_t[r][:, 4 * P + tok + o : 4 * P + tok + o + width],
+                            MULT,
+                        )
             return terms
 
-        def turn(b, terms, o):
-            dealt = ring4.tile([P, 4, P], F32, name="dealt")
-            for rows in ((0, 4),) if b < head else ((0, 2), (2, 4)):
-                turned = left.tile([P, BANK], F32, name=f"left{b if b < head else 1 + rows[0] // 2}")
-                for j in range(*rows):
-                    for r in range(2):
-                        nc.tensor.matmul(
-                            turned[:, P * j : P * (j + 1)], terms[j][r][:, o : o + P], ident[:],
-                            is_transpose=True, start=(r == 0), stop=(r == 1),
-                        )
-                nc.scalar.copy(
-                    dealt[:, :, 32 * rows[0] : 32 * rows[1]],
-                    turned[:, P * rows[0] : P * rows[1]].rearrange("p (m t) -> p t m", t=4),
-                )
-            backs[b] = bank("right")
+        def turn_rows(turned, terms, o, rows):
+            for j in range(*rows):
+                for r in range(2):
+                    nc.tensor.matmul(
+                        turned[:, P * j : P * (j + 1)], terms[j][r][:, o : o + P], ident[:],
+                        is_transpose=True, start=(r == 0), stop=(r == 1),
+                    )
+
+        def deal_rows(dealt, turned, rows):
+            nc.scalar.copy(
+                dealt[:, :, 32 * rows[0] : 32 * rows[1]],
+                turned[:, P * rows[0] : P * rows[1]].rearrange("p (m t) -> p t m", t=4),
+            )
+
+        def turn_back(b, dealt):
+            backs[b] = bank((2, 3, 4, 0, 1)[b % 5])
             for t in range(4):
                 nc.tensor.transpose(backs[b][:, P * t : P * (t + 1)], dealt[:, t, :], ident[:])
 
-        def finish(b):
-            cols = slice(b * P, (b + 1) * P)
-            rounded = held(f"rounded{b}", [P, 4 * P], BF16)
+        def round_block(b):
             nc.scalar.copy(
-                rounded[:].rearrange("p (w t) -> p w t", t=4),
+                rounded[:, 4 * P * b : 4 * P * (b + 1)].rearrange("p (w t) -> p w t", t=4),
                 backs[b][:].rearrange("p (t w) -> p w t", t=4),
             )
+
+        def store_block(b):
             result = held(f"result{b}", [P, 4, P], F32)
             nc.scalar.copy(result[:], backs[b][:].rearrange("p (t w) -> p t w", t=4))
-            nc.vector.quantize_mx(out=out_codes[:, cols].bitcast(FP8X4), scales=out_plane[:, cols], in_=rounded[:])
-            nc.sync.dma_start(out_rows[:, :, cols], result[:])
-            if b == blocks - 2:
-                nc.sync.dma_start(out_words[:, : T - P], out_codes[:, : T - P].bitcast(I32))
+            nc.sync.dma_start(out_rows[:, :, b * P : (b + 1) * P], result[:])
+
+        def finish(b):
+            round_block(b)
+            store_block(b)
 
         def finish_last(b, terms):
             tok = b * P
             cols = slice(tok, T)
             dealt = held("dealt_pairs", [P, 2, P, 2], BF16)
-            for rows in ((0, 3), (3, 4)):
-                turned = left.tile([P, BANK], F32, name=f"left{1 + rows[0] // 2}")
-                for j in range(*rows):
-                    for r in range(2):
-                        nc.tensor.matmul(
-                            turned[:, P * j : P * (j + 1)], terms[j][r], ident[:],
-                            is_transpose=True, start=(r == 0), stop=(r == 1),
-                        )
+            for rows, which in (((0, 3), 5), ((3, 4), 6)):
+                turned = bank(which)
+                turn_rows(turned, terms, 0, rows)
                 nc.scalar.copy(
                     dealt[:, :, 32 * rows[0] : 32 * rows[1], :],
                     turned[:, P * rows[0] : P * rows[1]].rearrange("p (m u e) -> p u m e", u=2, e=2),
                 )
             words = dealt[:].rearrange("p u m e -> p (u m e)").bitcast(F32)
-            back = bank("right")
+            back = bank(7)
             for u in range(2):
                 nc.tensor.transpose(back[:, P * u : P * (u + 1)], words[:, P * u : P * (u + 1)], ident[:])
             finish(b - 1)
             result = held("result_last", [P, 4, P], F32)
-            for j in range(4):
-                nc.vector.tensor_tensor(result[:, j, :], terms[j][0], terms[j][1], ADD)
+            nc.vector.tensor_tensor(
+                result[:].rearrange("p j w -> p (j w)"),
+                gate_t[0][:, 4 * P : 8 * P], gate_t[1][:, 4 * P : 8 * P], ADD,
+            )
             nc.sync.dma_start(out_0.rearrange("(j p) w -> p j w", j=4)[:, :, cols], result[:])
-            rounded = held("rounded_last", [P, 4 * P], BF16)
             nc.scalar.copy(
-                rounded[:].bitcast(F32).rearrange("p (w u) -> p w u", u=2),
+                rounded[:, 4 * tok :].bitcast(F32).rearrange("p (w u) -> p w u", u=2),
                 back[:, : 2 * P].rearrange("p (u w) -> p w u", u=2),
             )
-            nc.vector.quantize_mx(out=out_codes[:, cols].bitcast(FP8X4), scales=out_plane[:, cols], in_=rounded[:])
-            nc.sync.dma_start(out_words[:, cols], out_codes[:, cols].bitcast(I32))
 
+        halves = ((0, 2), (2, 4))
         terms = combine(0, head * P)
-        for b in range(blocks - 1):
-            if b >= head:
-                terms = combine(b, P)
-            turn(b, terms, b * P if b < head else 0)
-            if b:
-                finish(b - 1)
-        finish_last(blocks - 1, combine(blocks - 1, P))
+        dealts = [ring4.tile([P, 4, P], F32, name="dealt") for b in range(head)]
+        turneds = [bank(5 + b) for b in range(head)]
+        for rows in halves:
+            for b in range(head):
+                turn_rows(turneds[b], terms, b * P, rows)
+                deal_rows(dealts[b], turneds[b], rows)
+                if rows[1] == 4:
+                    turn_back(b, dealts[b])
+                    if b:
+                        finish(b - 1)
+        for b in range(head, blocks - 1):
+            terms = combine(b, P)
+            dealt = ring4.tile([P, 4, P], F32, name="dealt")
+            for rows in halves:
+                turned = bank(5 + rows[0] // 2)
+                turn_rows(turned, terms, 0, rows)
+                deal_rows(dealt, turned, rows)
+            turn_back(b, dealt)
+            finish(b - 1)
+        last_terms = combine(blocks - 1, P)
+        finish_last(blocks - 1, last_terms)
+        out_codes = held("out_codes", [P, T], U32, tag="y3")
+        out_plane = held("out_plane", [P, T], U8, tag="y2")
+        for t0, t1 in ((0, 4 * P), (4 * P, 6 * P), (6 * P, 7 * P), (7 * P, T)):
+            nc.vector.quantize_mx(
+                out=out_codes[:, t0:t1].bitcast(FP8X4), scales=out_plane[:, t0:t1], in_=rounded[:, 4 * t0 : 4 * t1]
+            )
+            if t1 in (6 * P, T):
+                s0 = 0 if t1 < T else 6 * P
+                nc.sync.dma_start(out_words[:, s0:t1], out_codes[:, s0:t1].bitcast(I32))
         scale_rows = out_2[0].bitcast(I32).rearrange("(q r) n -> r q n", r=4)
         for r in range(4):
             nc.scalar.dma_start(scale_rows[r], out_plane[r:P:32, :].bitcast(I32))

@@ -22,9 +22,12 @@ MAX = mybir.AluOpType.max
 
 P = 128
 BANK = 512
+STEP = BANK // 2
 CHUNK = 256
 LAG = 3
 GPSIMD_STEPS = (4, 5, 6)
+HEAD = 3
+SPARE = 4
 
 
 def tile_moe_sup_glu_relu_kernel(
@@ -34,7 +37,7 @@ def tile_moe_sup_glu_relu_kernel(
     nc = tc.nc
     with ExitStack() as ctx:
         keep = ctx.enter_context(tc.tile_pool(name="keep", bufs=1))
-        ring4 = ctx.enter_context(tc.tile_pool(name="ring4", bufs=4))
+        ring = ctx.enter_context(tc.tile_pool(name="ring", bufs=HEAD + 1))
         psum = ctx.enter_context(tc.psum_pool(name="psum", bufs=1))
 
         def held(name, shape, dtype, tag=""):
@@ -56,24 +59,20 @@ def tile_moe_sup_glu_relu_kernel(
         xs = held("xs", [P, T], U8)
         w2s = held("w2s", [P, E * N], U8)
         nc.gpsimd.memset(w3s_raw[:].bitcast(I32), 0)
-        nc.gpsimd.memset(xs[:].bitcast(I32), 0)
         nc.vector.memset(w1s_raw[:].bitcast(I32), 0)
-        nc.vector.memset(w2s[:].bitcast(I32), 0)
 
         w3_raw = held("w3_raw", [P, H], I32)
         w1_raw = held("w1_raw", [P, H], I32)
-        xw_dram = x_words[0].rearrange("p t d -> p (t d)").bitcast(I32)
         xw = held("xw", [P, T], I32)
         xs_rows = x_scales[0].bitcast(I32).rearrange("(q r) n -> r q n", r=4)
-        w1s_rows = w1_scales[0].bitcast(I32).rearrange("(q r) n -> r q n", r=4)
         load_scale_rows(xs, xs_rows, (3,), nc.gpsimd)
         nc.sync.dma_start(w3_raw[:], w3_words[0].rearrange("p i d -> p (i d)").bitcast(I32))
         load_scale_rows(w3s_raw, w3_scales[0].bitcast(I32).rearrange("(q r) n -> r q n", r=4))
         load_scale_rows(xs, xs_rows, (0, 1))
-        nc.sync.dma_start(xw[:], xw_dram)
+        nc.sync.dma_start(xw[:], x_words[0].rearrange("p t d -> p (t d)").bitcast(I32))
         load_scale_rows(xs, xs_rows, (2,))
         nc.sync.dma_start(w1_raw[:], w1_words[0].rearrange("p i d -> p (i d)").bitcast(I32))
-        load_scale_rows(w1s_raw, w1s_rows)
+        load_scale_rows(w1s_raw, w1_scales[0].bitcast(I32).rearrange("(q r) n -> r q n", r=4))
         offs_t = held("offs_t", [P, S // 16], U16)
         nc.sync.dma_start(offs_t[:], offs)
         w2w = [held(f"w2w{a}", [P, 4 * 2 * N], U8) for a in range(4)]
@@ -86,51 +85,40 @@ def tile_moe_sup_glu_relu_kernel(
         pos_t = [held(f"pos{r}", [P, T // 16], U16) for r in range(2)]
         nc.sync.dma_start(pos_t[0][:], pos1)
         nc.sync.dma_start(pos_t[1][:], pos2)
-        gate_t = [held(f"gate{r}", [P, 4 * P + T], F32) for r in range(2)]
+        gate_t = [held(f"gate{r}", [P, SPARE * P + T], F32) for r in range(2)]
         for r in range(2):
-            nc.sync.dma_start(gate_t[r][:, 4 * P :], gate[r])
+            nc.sync.dma_start(gate_t[r][:, SPARE * P :], gate[r])
 
-        warm = bank(7)
-        for i in range(3):
-            nc.tensor.matmul_mx(
-                out=warm[:], lhsT=w3_raw[:, :P].bitcast(FP8X4), lhsT_scale=w3s_raw[:, :P],
-                rhs=w3_raw[:].bitcast(FP8X4), rhs_scale=w3s_raw[:], start=(i == 0), stop=(i == 2),
-            )
         w3 = held("w3", [P, H], I32)
         w1 = held("w1", [P, H], I32)
         w3s = held("w3s", [P, H], U8)
         w1s = held("w1s", [P, H], U8)
-        for pair in (((w3, w3_raw, 4), (w3s, w3s_raw, 16)), ((w1, w1_raw, 4), (w1s, w1s_raw, 16))):
+        for operand in (((w3, w3_raw, 4), (w3s, w3s_raw, 16)), ((w1, w1_raw, 4), (w1s, w1s_raw, 16))):
             for u in range(2):
-                for dst, src, run in pair:
+                for dst, src, run in operand:
                     nc.vector.tensor_copy(
                         dst[:].rearrange("p (t c i) -> p c t i", t=4, i=run)[:, :, 2 * u : 2 * u + 2, :],
                         src[:].rearrange("p (c i t) -> p c t i", t=4, i=run)[:, :, 2 * u : 2 * u + 2, :],
                     )
 
-        ident = held("ident", [P, P], F32, tag="w3_raw")
-        make_identity(nc, ident[:])
         h = [held(f"h{u}", [P, 2 * T], BF16) for u in range(2)]
-        Q = BANK // 2
 
         def first_product(w, ws, u, tok, acc):
             for e in range(2):
                 cols = slice(P * (2 * u + e), P * (2 * u + e + 1))
                 nc.tensor.matmul_mx(
-                    out=acc[:, Q * e : Q * (e + 1)],
+                    out=acc[:, STEP * e : STEP * (e + 1)],
                     lhsT=w[:, cols].bitcast(FP8X4),
                     lhsT_scale=ws[:, cols],
-                    rhs=xw[:, tok : tok + Q].bitcast(FP8X4),
-                    rhs_scale=xs[:, tok : tok + Q],
+                    rhs=xw[:, tok : tok + STEP].bitcast(FP8X4),
+                    rhs_scale=xs[:, tok : tok + STEP],
                     start=True,
                     stop=True,
                 )
             return acc[:].rearrange("p (e t) -> p t e", e=2)
 
-        steps = [
-            (u, tok) for u in range(2) for tok in range(0, T, Q)
-        ]
-        a3_sb = [held(f"a3_sb{i}", [P, Q, 2], F32) for i in range(len(steps))]
+        steps = [(u, tok) for u in range(2) for tok in range(0, T, STEP)]
+        a3_sb = [held(f"a3_sb{i}", [P, STEP, 2], F32) for i in range(len(steps))]
 
         def linear_half(i):
             nc.scalar.copy(a3_sb[i][:], first_product(w3, w3s, *steps[i], bank(i % 4)))
@@ -138,9 +126,9 @@ def tile_moe_sup_glu_relu_kernel(
         def gated_half(i):
             u, tok = steps[i]
             a1 = first_product(w1, w1s, u, tok, bank(4 + i % 4))
-            out = h[u][:, 2 * tok : 2 * (tok + Q)].rearrange("p (t e) -> p t e", e=2)
+            out = h[u][:, 2 * tok : 2 * (tok + STEP)].rearrange("p (t e) -> p t e", e=2)
             if i in GPSIMD_STEPS:
-                a1_sb = held(f"a1_sb{i}", [P, Q, 2], F32)
+                a1_sb = held(f"a1_sb{i}", [P, STEP, 2], F32)
                 nc.scalar.activation(a1_sb[:], a1, RELU)
                 nc.gpsimd.tensor_tensor(out, a1_sb[:], a3_sb[i][:], MULT)
             else:
@@ -148,13 +136,17 @@ def tile_moe_sup_glu_relu_kernel(
                     out=out, in0=a1, scalar=0.0, in1=a3_sb[i][:], op0=MAX, op1=MULT,
                 )
 
-        for i in range(4):
+        half = len(steps) // 2
+        for i in range(half):
             linear_half(i)
-        for i in range(4):
+        for i in range(half):
             gated_half(i)
-        for i in range(4, 8):
+        for i in range(half, len(steps)):
             linear_half(i)
             gated_half(i)
+
+        ident = held("ident", [P, P], F32, tag=f"a1_sb{GPSIMD_STEPS[-1]}")
+        make_identity(nc, ident[:])
 
         chunks = S // CHUNK
         y = [held(f"y{j}", [P, S], F32) for j in range(4)]
@@ -162,7 +154,7 @@ def tile_moe_sup_glu_relu_kernel(
         codes = {}
         planes = {}
         pairs = held("pairs", [P, (chunks + LAG) * CHUNK], U32)
-        rows = pairs[:].rearrange("p (r s) -> p r s", s=CHUNK)
+        pair_rows = pairs[:].rearrange("p (r s) -> p r s", s=CHUNK)
 
         def slots(s0, n):
             return offs_t[:, s0 // 16 : (s0 + n) // 16]
@@ -173,13 +165,15 @@ def tile_moe_sup_glu_relu_kernel(
                 both = pairs[:, (2 + LAG) * CHUNK : (4 + LAG) * CHUNK]
                 woven[c] = both.bitcast(BF16)
                 for u in range(2):
-                    nc.vector.tensor_copy(both.rearrange("p (s u) -> p s u", u=2)[:, :, u], h[u][:].bitcast(U32).indirect(lst))
+                    nc.vector.tensor_copy(
+                        both.rearrange("p (s u) -> p s u", u=2)[:, :, u], h[u][:].bitcast(U32).indirect(lst)
+                    )
             else:
                 woven[c] = held(f"woven{c}", [P, 4 * CHUNK], BF16)[:]
-                nc.vector.tensor_copy(rows[:, c + LAG, :], h[1][:].bitcast(U32).indirect(lst))
+                nc.vector.tensor_copy(pair_rows[:, c + LAG, :], h[1][:].bitcast(U32).indirect(lst))
                 nc.scalar.copy(
                     woven[c].bitcast(U32).rearrange("p (s u) -> p s u", u=2),
-                    rows[:, c : c + LAG + 1 : LAG, :].rearrange("p u s -> p s u"),
+                    pair_rows[:, c : c + LAG + 1 : LAG, :].rearrange("p u s -> p s u"),
                 )
 
         def quantise(c):
@@ -187,24 +181,25 @@ def tile_moe_sup_glu_relu_kernel(
             planes[c] = held(f"planes{c}", [P, CHUNK], U8)
             nc.vector.quantize_mx(out=codes[c][:].bitcast(FP8X4), scales=planes[c][:], in_=woven[c])
 
-        def second_product(j, s0, n, b):
-            acc = bank(b)
+        def second_product(j, s0, n, which):
+            acc = bank(which)
             for s in range(s0, s0 + n, C):
                 e = s // C
-                g, o = divmod(s, CHUNK)
+                c, o = divmod(s, CHUNK)
                 w0 = (e % 4) * 2 * N + 2 * P * j
                 nc.tensor.matmul_mx(
                     out=acc[:, s - s0 : s - s0 + C],
                     lhsT=w2w[e // 4][:, w0 : w0 + 2 * P].bitcast(FP4X4),
                     lhsT_scale=w2s[:, e * N + P * j : e * N + P * (j + 1)],
-                    rhs=codes[g][:, o : o + C].bitcast(FP8X4),
-                    rhs_scale=planes[g][:, o : o + C],
+                    rhs=codes[c][:, o : o + C].bitcast(FP8X4),
+                    rhs_scale=planes[c][:, o : o + C],
                     start=True,
                     stop=True,
                 )
             return y[j][:, s0 : s0 + n], acc[:, :n]
 
-        for s0, n in ((5 * CHUNK, 3 * CHUNK), (3 * CHUNK, 2 * CHUNK), (CHUNK, 2 * CHUNK)):
+        for c0, c1 in ((5, 8), (3, 5), (1, 3)):
+            s0, n = c0 * CHUNK, (c1 - c0) * CHUNK
             nc.vector.tensor_copy(pairs[:, s0 : s0 + n], h[0][:].bitcast(U32).indirect(slots(s0, n)))
         for c in range(chunks - 1, 0, -1):
             gather(c)
@@ -219,17 +214,17 @@ def tile_moe_sup_glu_relu_kernel(
         quantise(0)
         nc.scalar.copy(*second_product(0, CHUNK, CHUNK, 7))
         nc.scalar.copy(*second_product(0, 0, CHUNK, 2))
-        for pair in by_vector:
-            nc.vector.tensor_copy(*pair)
+        for copy_args in by_vector:
+            nc.vector.tensor_copy(*copy_args)
         rest = [(1, 1), (1, 0)] + [(j, q) for j in (2, 3) for q in (3, 2, 1, 0)]
-        for (j, q), b in zip(rest, (3, 4, 5, 6, 7, 2, 3, 4, 0, 1)):
-            nc.scalar.copy(*second_product(j, q * BANK, BANK, b))
+        for (j, q), which in zip(rest, (3, 4, 5, 6, 7, 2, 3, 4, 0, 1)):
+            nc.scalar.copy(*second_product(j, q * BANK, BANK, which))
 
         rounded = held("rounded", [P, 4 * T], BF16)
         out_rows = out_0.rearrange("(p t) w -> p t w", t=4)
         out_words = out_1[0].rearrange("p t d -> p (t d)").bitcast(I32)
         blocks = T // P
-        head = 3
+        last = blocks - 1
         backs = {}
 
         def combine(b, n):
@@ -238,32 +233,33 @@ def tile_moe_sup_glu_relu_kernel(
                 terms = [[held(f"term{j}_{r}", [P, n], F32)[:] for r in range(2)] for j in range(3)]
                 terms.append([g[:, :n] for g in gate_t])
             else:
-                places = [4 * (b % 2) + j for j in range(3)] + [3 if b in (3, 5) else 7]
+                places = [4 * (b % 2) + j for j in range(3)] + [3 if b % 2 and b < last else 7]
                 terms = [[g[:, P * place : P * (place + 1)] for g in gate_t] for place in places]
             for j in range(4):
                 width = P if j == 3 else n
                 for o in range(0, n, width):
+                    g0 = SPARE * P + tok + o
                     for r in range(2):
                         nc.vector.tensor_tensor(
                             terms[j][r][:, o : o + width],
                             y[j][:].indirect(pos_t[r][:, (tok + o) // 16 : (tok + o + width) // 16]),
-                            gate_t[r][:, 4 * P + tok + o : 4 * P + tok + o + width],
+                            gate_t[r][:, g0 : g0 + width],
                             MULT,
                         )
             return terms
 
-        def turn_rows(turned, terms, o, rows):
-            for j in range(*rows):
+        def turn_rows(turned, terms, o, tiles):
+            for j in range(*tiles):
                 for r in range(2):
                     nc.tensor.matmul(
                         turned[:, P * j : P * (j + 1)], terms[j][r][:, o : o + P], ident[:],
                         is_transpose=True, start=(r == 0), stop=(r == 1),
                     )
 
-        def deal_rows(dealt, turned, rows):
+        def deal_rows(dealt, turned, tiles):
             nc.scalar.copy(
-                dealt[:, :, 32 * rows[0] : 32 * rows[1]],
-                turned[:, P * rows[0] : P * rows[1]].rearrange("p (m t) -> p t m", t=4),
+                dealt[:, :, 32 * tiles[0] : 32 * tiles[1]],
+                turned[:, P * tiles[0] : P * tiles[1]].rearrange("p (m t) -> p t m", t=4),
             )
 
         def turn_back(b, dealt):
@@ -271,80 +267,74 @@ def tile_moe_sup_glu_relu_kernel(
             for t in range(4):
                 nc.tensor.transpose(backs[b][:, P * t : P * (t + 1)], dealt[:, t, :], ident[:])
 
-        def round_block(b):
+        def finish(b):
             nc.scalar.copy(
                 rounded[:, 4 * P * b : 4 * P * (b + 1)].rearrange("p (w t) -> p w t", t=4),
                 backs[b][:].rearrange("p (t w) -> p w t", t=4),
             )
-
-        def store_block(b):
             result = held(f"result{b}", [P, 4, P], F32)
             nc.scalar.copy(result[:], backs[b][:].rearrange("p (t w) -> p t w", t=4))
             nc.sync.dma_start(out_rows[:, :, b * P : (b + 1) * P], result[:])
 
-        def finish(b):
-            round_block(b)
-            store_block(b)
-
-        def finish_last(b, terms):
-            tok = b * P
-            cols = slice(tok, T)
-            dealt = held("dealt_pairs", [P, 2, P, 2], BF16)
-            for rows, which in (((0, 3), 5), ((3, 4), 6)):
-                turned = bank(which)
-                turn_rows(turned, terms, 0, rows)
-                nc.scalar.copy(
-                    dealt[:, :, 32 * rows[0] : 32 * rows[1], :],
-                    turned[:, P * rows[0] : P * rows[1]].rearrange("p (m u e) -> p u m e", u=2, e=2),
-                )
-            words = dealt[:].rearrange("p u m e -> p (u m e)").bitcast(F32)
-            back = bank(7)
-            for u in range(2):
-                nc.tensor.transpose(back[:, P * u : P * (u + 1)], words[:, P * u : P * (u + 1)], ident[:])
-            finish(b - 1)
-            result = held("result_last", [P, 4, P], F32)
-            nc.vector.tensor_tensor(
-                result[:].rearrange("p j w -> p (j w)"),
-                gate_t[0][:, 4 * P : 8 * P], gate_t[1][:, 4 * P : 8 * P], ADD,
-            )
-            nc.sync.dma_start(out_0.rearrange("(j p) w -> p j w", j=4)[:, :, cols], result[:])
-            nc.scalar.copy(
-                rounded[:, 4 * tok :].bitcast(F32).rearrange("p (w u) -> p w u", u=2),
-                back[:, : 2 * P].rearrange("p (u w) -> p w u", u=2),
-            )
-
         halves = ((0, 2), (2, 4))
-        terms = combine(0, head * P)
-        dealts = [ring4.tile([P, 4, P], F32, name="dealt") for b in range(head)]
-        turneds = [bank(5 + b) for b in range(head)]
-        for rows in halves:
-            for b in range(head):
-                turn_rows(turneds[b], terms, b * P, rows)
-                deal_rows(dealts[b], turneds[b], rows)
-                if rows[1] == 4:
+        terms = combine(0, HEAD * P)
+        dealts = [ring.tile([P, 4, P], F32, name="dealt") for b in range(HEAD)]
+        turneds = [bank(5 + b) for b in range(HEAD)]
+        for tiles in halves:
+            for b in range(HEAD):
+                turn_rows(turneds[b], terms, b * P, tiles)
+                deal_rows(dealts[b], turneds[b], tiles)
+                if tiles == halves[1]:
                     turn_back(b, dealts[b])
                     if b:
                         finish(b - 1)
-        for b in range(head, blocks - 1):
+        for b in range(HEAD, last):
             terms = combine(b, P)
-            dealt = ring4.tile([P, 4, P], F32, name="dealt")
-            for rows in halves:
-                turned = bank(5 + rows[0] // 2)
-                turn_rows(turned, terms, 0, rows)
-                deal_rows(dealt, turned, rows)
+            dealt = ring.tile([P, 4, P], F32, name="dealt")
+            for which, tiles in zip((5, 6), halves):
+                turned = bank(which)
+                turn_rows(turned, terms, 0, tiles)
+                deal_rows(dealt, turned, tiles)
             turn_back(b, dealt)
             finish(b - 1)
-        last_terms = combine(blocks - 1, P)
-        finish_last(blocks - 1, last_terms)
+
+        terms = combine(last, P)
+        tok = last * P
+        dealt_pairs = held("dealt_pairs", [P, 2, P, 2], BF16)
+        for which, tiles in zip((5, 6), ((0, 3), (3, 4))):
+            turned = bank(which)
+            turn_rows(turned, terms, 0, tiles)
+            nc.scalar.copy(
+                dealt_pairs[:, :, 32 * tiles[0] : 32 * tiles[1], :],
+                turned[:, P * tiles[0] : P * tiles[1]].rearrange("p (m u e) -> p u m e", u=2, e=2),
+            )
+        pair_words = dealt_pairs[:].rearrange("p u m e -> p (u m e)").bitcast(F32)
+        back = bank(7)
+        for u in range(2):
+            nc.tensor.transpose(back[:, P * u : P * (u + 1)], pair_words[:, P * u : P * (u + 1)], ident[:])
+        finish(last - 1)
+        result_last = held("result_last", [P, 4, P], F32)
+        nc.vector.tensor_tensor(
+            result_last[:].rearrange("p j w -> p (j w)"),
+            gate_t[0][:, 4 * P : 8 * P], gate_t[1][:, 4 * P : 8 * P], ADD,
+        )
+        nc.sync.dma_start(out_0.rearrange("(j p) w -> p j w", j=4)[:, :, tok:], result_last[:])
+        nc.scalar.copy(
+            rounded[:, 4 * tok :].bitcast(F32).rearrange("p (w u) -> p w u", u=2),
+            back[:, : 2 * P].rearrange("p (u w) -> p w u", u=2),
+        )
+
         out_codes = held("out_codes", [P, T], U32, tag="y3")
         out_plane = held("out_plane", [P, T], U8, tag="y2")
-        for t0, t1 in ((0, 4 * P), (4 * P, 6 * P), (6 * P, 7 * P), (7 * P, T)):
-            nc.vector.quantize_mx(
-                out=out_codes[:, t0:t1].bitcast(FP8X4), scales=out_plane[:, t0:t1], in_=rounded[:, 4 * t0 : 4 * t1]
-            )
-            if t1 in (6 * P, T):
-                s0 = 0 if t1 < T else 6 * P
-                nc.sync.dma_start(out_words[:, s0:t1], out_codes[:, s0:t1].bitcast(I32))
+        for parts in (((0, 4), (4, 6)), ((6, 7), (7, 8))):
+            for b0, b1 in parts:
+                cols = slice(b0 * P, b1 * P)
+                nc.vector.quantize_mx(
+                    out=out_codes[:, cols].bitcast(FP8X4), scales=out_plane[:, cols],
+                    in_=rounded[:, 4 * b0 * P : 4 * b1 * P],
+                )
+            cols = slice(parts[0][0] * P, parts[-1][1] * P)
+            nc.sync.dma_start(out_words[:, cols], out_codes[:, cols].bitcast(I32))
         scale_rows = out_2[0].bitcast(I32).rearrange("(q r) n -> r q n", r=4)
         for r in range(4):
             nc.scalar.dma_start(scale_rows[r], out_plane[r:P:32, :].bitcast(I32))

@@ -63,16 +63,20 @@ def tile_moe_sup_glu_relu_kernel(
 
         w3_raw = held("w3_raw", [P, H], I32)
         w1_raw = held("w1_raw", [P, H], I32)
-        xw = held("xw", [P, T], I32)
+        xw = [held(f"xw{a}", [P, T // 2], I32) for a in range(2)]
         xs_rows = x_scales[0].bitcast(I32).rearrange("(q r) n -> r q n", r=4)
+        w1s_rows = w1_scales[0].bitcast(I32).rearrange("(q r) n -> r q n", r=4)
+        x_all = x_words[0].rearrange("p t d -> p (t d)").bitcast(I32)
         load_scale_rows(xs, xs_rows, (3,), nc.gpsimd)
-        nc.sync.dma_start(w3_raw[:], w3_words[0].rearrange("p i d -> p (i d)").bitcast(I32))
+        load_scale_rows(xs, xs_rows, (0,))
         load_scale_rows(w3s_raw, w3_scales[0].bitcast(I32).rearrange("(q r) n -> r q n", r=4))
-        load_scale_rows(xs, xs_rows, (0, 1))
-        nc.sync.dma_start(xw[:], x_words[0].rearrange("p t d -> p (t d)").bitcast(I32))
+        load_scale_rows(xs, xs_rows, (1,))
+        nc.sync.dma_start(w3_raw[:], w3_words[0].rearrange("p i d -> p (i d)").bitcast(I32))
+        nc.sync.dma_start(xw[0][:], x_all[:, : T // 2])
         load_scale_rows(xs, xs_rows, (2,))
         nc.sync.dma_start(w1_raw[:], w1_words[0].rearrange("p i d -> p (i d)").bitcast(I32))
-        load_scale_rows(w1s_raw, w1_scales[0].bitcast(I32).rearrange("(q r) n -> r q n", r=4))
+        load_scale_rows(w1s_raw, w1s_rows)
+        nc.sync.dma_start(xw[1][:], x_all[:, T // 2 :])
         offs_t = held("offs_t", [P, S // 16], U16)
         nc.sync.dma_start(offs_t[:], offs)
         w2w = [held(f"w2w{a}", [P, 4 * 2 * N], U8) for a in range(4)]
@@ -110,22 +114,22 @@ def tile_moe_sup_glu_relu_kernel(
                     out=acc[:, STEP * e : STEP * (e + 1)],
                     lhsT=w[:, cols].bitcast(FP8X4),
                     lhsT_scale=ws[:, cols],
-                    rhs=xw[:, tok : tok + STEP].bitcast(FP8X4),
+                    rhs=xw[tok // (T // 2)][:, tok % (T // 2) : tok % (T // 2) + STEP].bitcast(FP8X4),
                     rhs_scale=xs[:, tok : tok + STEP],
                     start=True,
                     stop=True,
                 )
             return acc[:].rearrange("p (e t) -> p t e", e=2)
 
-        steps = [(u, tok) for u in range(2) for tok in range(0, T, STEP)]
+        steps = [(u, (tok + u * T // 2) % T) for u in range(2) for tok in range(0, T, STEP)]
         a3_sb = [held(f"a3_sb{i}", [P, STEP, 2], F32) for i in range(len(steps))]
 
         def linear_half(i):
-            nc.scalar.copy(a3_sb[i][:], first_product(w3, w3s, *steps[i], bank(i % 4)))
+            nc.scalar.copy(a3_sb[i][:], first_product(w3, w3s, *steps[i], bank((0, 1, 2, 3, 0, 4, 2, 6)[i])))
 
         def gated_half(i):
             u, tok = steps[i]
-            a1 = first_product(w1, w1s, u, tok, bank(4 + i % 4))
+            a1 = first_product(w1, w1s, u, tok, bank((4, 5, 6, 7, 1, 5, 3, 7)[i]))
             out = h[u][:, 2 * tok : 2 * (tok + STEP)].rearrange("p (t e) -> p t e", e=2)
             if i in GPSIMD_STEPS:
                 a1_sb = held(f"a1_sb{i}", [P, STEP, 2], F32)
@@ -136,13 +140,12 @@ def tile_moe_sup_glu_relu_kernel(
                     out=out, in0=a1, scalar=0.0, in1=a3_sb[i][:], op0=MAX, op1=MULT,
                 )
 
-        half = len(steps) // 2
-        for i in range(half):
-            linear_half(i)
-        for i in range(half):
-            gated_half(i)
-        for i in range(half, len(steps)):
-            linear_half(i)
+        linear_half(0)
+        for i in range(len(steps)):
+            if i + 1 == 1:
+                linear_half(1)
+            if i > 1:
+                linear_half(i)
             gated_half(i)
 
         ident = held("ident", [P, P], F32, tag=f"a1_sb{GPSIMD_STEPS[-1]}")
@@ -267,14 +270,19 @@ def tile_moe_sup_glu_relu_kernel(
             for t in range(4):
                 nc.tensor.transpose(backs[b][:, P * t : P * (t + 1)], dealt[:, t, :], ident[:])
 
+        results = {}
+
+        def store(b):
+            results[b] = held(f"result{b}", [P, 4, P], F32)
+            nc.scalar.copy(results[b][:], backs[b][:].rearrange("p (t w) -> p t w", t=4))
+            nc.sync.dma_start(out_rows[:, :, b * P : (b + 1) * P], results[b][:])
+
         def finish(b):
             nc.scalar.copy(
                 rounded[:, 4 * P * b : 4 * P * (b + 1)].rearrange("p (w t) -> p w t", t=4),
                 backs[b][:].rearrange("p (t w) -> p w t", t=4),
             )
-            result = held(f"result{b}", [P, 4, P], F32)
-            nc.scalar.copy(result[:], backs[b][:].rearrange("p (t w) -> p t w", t=4))
-            nc.sync.dma_start(out_rows[:, :, b * P : (b + 1) * P], result[:])
+            store(b)
 
         halves = ((0, 2), (2, 4))
         terms = combine(0, HEAD * P)
@@ -298,6 +306,7 @@ def tile_moe_sup_glu_relu_kernel(
             turn_back(b, dealt)
             finish(b - 1)
 
+        store(last - 1)
         terms = combine(last, P)
         tok = last * P
         dealt_pairs = held("dealt_pairs", [P, 2, P, 2], BF16)
@@ -312,7 +321,24 @@ def tile_moe_sup_glu_relu_kernel(
         back = bank(7)
         for u in range(2):
             nc.tensor.transpose(back[:, P * u : P * (u + 1)], pair_words[:, P * u : P * (u + 1)], ident[:])
-        finish(last - 1)
+        out_codes = held("out_codes", [P, T], U32, tag="y3")
+        out_plane = held("out_plane", [P, T], U8, tag="y2")
+
+        def planes_of(parts):
+            for b0, b1 in parts:
+                cols = slice(b0 * P, b1 * P)
+                nc.vector.quantize_mx(
+                    out=out_codes[:, cols].bitcast(FP8X4), scales=out_plane[:, cols],
+                    in_=rounded[:, 4 * b0 * P : 4 * b1 * P],
+                )
+            cols = slice(parts[0][0] * P, parts[-1][1] * P)
+            nc.sync.dma_start(out_words[:, cols], out_codes[:, cols].bitcast(I32))
+
+        planes_of(((0, 4),))
+        nc.vector.tensor_copy(
+            rounded[:, 4 * P * (last - 1) : 4 * P * last].rearrange("p (c i t) -> p c t i", t=4, i=4),
+            results[last - 1][:].rearrange("p t (c i) -> p c t i", i=4),
+        )
         result_last = held("result_last", [P, 4, P], F32)
         nc.vector.tensor_tensor(
             result_last[:].rearrange("p j w -> p (j w)"),
@@ -323,18 +349,8 @@ def tile_moe_sup_glu_relu_kernel(
             rounded[:, 4 * tok :].bitcast(F32).rearrange("p (w u) -> p w u", u=2),
             back[:, : 2 * P].rearrange("p (u w) -> p w u", u=2),
         )
-
-        out_codes = held("out_codes", [P, T], U32, tag="y3")
-        out_plane = held("out_plane", [P, T], U8, tag="y2")
-        for parts in (((0, 4), (4, 6)), ((6, 7), (7, 8))):
-            for b0, b1 in parts:
-                cols = slice(b0 * P, b1 * P)
-                nc.vector.quantize_mx(
-                    out=out_codes[:, cols].bitcast(FP8X4), scales=out_plane[:, cols],
-                    in_=rounded[:, 4 * b0 * P : 4 * b1 * P],
-                )
-            cols = slice(parts[0][0] * P, parts[-1][1] * P)
-            nc.sync.dma_start(out_words[:, cols], out_codes[:, cols].bitcast(I32))
+        planes_of(((4, 6), (6, 7)))
+        planes_of(((7, 8),))
         scale_rows = out_2[0].bitcast(I32).rearrange("(q r) n -> r q n", r=4)
         for r in range(4):
-            nc.scalar.dma_start(scale_rows[r], out_plane[r:P:32, :].bitcast(I32))
+            (nc.scalar if r < 3 else nc.sync).dma_start(scale_rows[r], out_plane[r:P:32, :].bitcast(I32))

@@ -23,6 +23,7 @@ MAX = mybir.AluOpType.max
 P = 128
 BANK = 512
 STEP = BANK // 2
+AHEAD = 2
 CHUNK = 256
 LAG = 3
 GPSIMD_STEPS = (4, 5, 6)
@@ -46,20 +47,20 @@ def tile_moe_sup_glu_relu_kernel(
         def bank(i):
             return psum.tile([P, BANK], F32, name=f"bank{i}")
 
-        def load_scale_rows(plane, rows, which=range(4), queue=nc.sync):
+        def load_scale_rows(plane, rows, which=range(4)):
             for r in which:
                 dst = plane[r:P:32, :].bitcast(I32)
                 src = rows[r]
                 if len(src.shape) == 3:
                     dst = dst.rearrange("q (e n) -> q e n", e=src.shape[1])
-                queue.dma_start(dst, src)
+                nc.sync.dma_start(dst, src)
 
         w3s_raw = held("w3s_raw", [P, H], U8)
         w1s_raw = held("w1s_raw", [P, H], U8)
         xs = held("xs", [P, T], U8)
         w2s = held("w2s", [P, E * N], U8)
         nc.gpsimd.memset(w3s_raw[:].bitcast(I32), 0)
-        nc.vector.memset(w1s_raw[:].bitcast(I32), 0)
+        nc.gpsimd.memset(w1s_raw[:].bitcast(I32), 0)
 
         w3_raw = held("w3_raw", [P, H], I32)
         w1_raw = held("w1_raw", [P, H], I32)
@@ -67,13 +68,11 @@ def tile_moe_sup_glu_relu_kernel(
         xs_rows = x_scales[0].bitcast(I32).rearrange("(q r) n -> r q n", r=4)
         w1s_rows = w1_scales[0].bitcast(I32).rearrange("(q r) n -> r q n", r=4)
         x_all = x_words[0].rearrange("p t d -> p (t d)").bitcast(I32)
-        load_scale_rows(xs, xs_rows, (3,), nc.gpsimd)
-        load_scale_rows(xs, xs_rows, (0,))
+        load_scale_rows(xs, xs_rows, (0, 1))
         load_scale_rows(w3s_raw, w3_scales[0].bitcast(I32).rearrange("(q r) n -> r q n", r=4))
-        load_scale_rows(xs, xs_rows, (1,))
         nc.sync.dma_start(w3_raw[:], w3_words[0].rearrange("p i d -> p (i d)").bitcast(I32))
         nc.sync.dma_start(xw[0][:], x_all[:, : T // 2])
-        load_scale_rows(xs, xs_rows, (2,))
+        load_scale_rows(xs, xs_rows, (2, 3))
         nc.sync.dma_start(w1_raw[:], w1_words[0].rearrange("p i d -> p (i d)").bitcast(I32))
         load_scale_rows(w1s_raw, w1s_rows)
         nc.sync.dma_start(xw[1][:], x_all[:, T // 2 :])
@@ -124,12 +123,14 @@ def tile_moe_sup_glu_relu_kernel(
         steps = [(u, (tok + u * T // 2) % T) for u in range(2) for tok in range(0, T, STEP)]
         a3_sb = [held(f"a3_sb{i}", [P, STEP, 2], F32) for i in range(len(steps))]
 
+        step_banks = [(i, 4 + i) for i in range(4)] + [(i, i + 1) for i in (0, 4, 2, 6)]
+
         def linear_half(i):
-            nc.scalar.copy(a3_sb[i][:], first_product(w3, w3s, *steps[i], bank((0, 1, 2, 3, 0, 4, 2, 6)[i])))
+            nc.scalar.copy(a3_sb[i][:], first_product(w3, w3s, *steps[i], bank(step_banks[i][0])))
 
         def gated_half(i):
             u, tok = steps[i]
-            a1 = first_product(w1, w1s, u, tok, bank((4, 5, 6, 7, 1, 5, 3, 7)[i]))
+            a1 = first_product(w1, w1s, u, tok, bank(step_banks[i][1]))
             out = h[u][:, 2 * tok : 2 * (tok + STEP)].rearrange("p (t e) -> p t e", e=2)
             if i in GPSIMD_STEPS:
                 a1_sb = held(f"a1_sb{i}", [P, STEP, 2], F32)
@@ -140,11 +141,10 @@ def tile_moe_sup_glu_relu_kernel(
                     out=out, in0=a1, scalar=0.0, in1=a3_sb[i][:], op0=MAX, op1=MULT,
                 )
 
-        linear_half(0)
+        for i in range(AHEAD):
+            linear_half(i)
         for i in range(len(steps)):
-            if i + 1 == 1:
-                linear_half(1)
-            if i > 1:
+            if i >= AHEAD:
                 linear_half(i)
             gated_half(i)
 
@@ -229,6 +229,7 @@ def tile_moe_sup_glu_relu_kernel(
         blocks = T // P
         last = blocks - 1
         backs = {}
+        results = {}
 
         def combine(b, n):
             tok = b * P
@@ -270,8 +271,6 @@ def tile_moe_sup_glu_relu_kernel(
             for t in range(4):
                 nc.tensor.transpose(backs[b][:, P * t : P * (t + 1)], dealt[:, t, :], ident[:])
 
-        results = {}
-
         def store(b):
             results[b] = held(f"result{b}", [P, 4, P], F32)
             nc.scalar.copy(results[b][:], backs[b][:].rearrange("p (t w) -> p t w", t=4))
@@ -307,6 +306,7 @@ def tile_moe_sup_glu_relu_kernel(
             finish(b - 1)
 
         store(last - 1)
+
         terms = combine(last, P)
         tok = last * P
         dealt_pairs = held("dealt_pairs", [P, 2, P, 2], BF16)
@@ -321,6 +321,7 @@ def tile_moe_sup_glu_relu_kernel(
         back = bank(7)
         for u in range(2):
             nc.tensor.transpose(back[:, P * u : P * (u + 1)], pair_words[:, P * u : P * (u + 1)], ident[:])
+
         out_codes = held("out_codes", [P, T], U32, tag="y3")
         out_plane = held("out_plane", [P, T], U8, tag="y2")
 

@@ -25,10 +25,11 @@ BANK = 512
 STEP = BANK // 2
 AHEAD = 2
 CHUNK = 256
-LAG = 3
-GPSIMD_STEPS = (4, 5, 6)
-HEAD = 3
-SPARE = 4
+GPSIMD_STEPS = (4, 5)
+EARLY = 4
+OWN = 2
+ROUNDED_BY_SCALAR = (3, 4)
+COPY = mybir.ActivationFunctionType.Copy
 
 
 def tile_moe_sup_glu_relu_kernel(
@@ -38,7 +39,7 @@ def tile_moe_sup_glu_relu_kernel(
     nc = tc.nc
     with ExitStack() as ctx:
         keep = ctx.enter_context(tc.tile_pool(name="keep", bufs=1))
-        ring = ctx.enter_context(tc.tile_pool(name="ring", bufs=HEAD + 1))
+        ring = ctx.enter_context(tc.tile_pool(name="ring", bufs=4))
         psum = ctx.enter_context(tc.psum_pool(name="psum", bufs=1))
 
         def held(name, shape, dtype, tag=""):
@@ -88,9 +89,13 @@ def tile_moe_sup_glu_relu_kernel(
         pos_t = [held(f"pos{r}", [P, T // 16], U16) for r in range(2)]
         nc.sync.dma_start(pos_t[0][:], pos1)
         nc.sync.dma_start(pos_t[1][:], pos2)
-        gate_t = [held(f"gate{r}", [P, SPARE * P + T], F32) for r in range(2)]
+        gate_t = [held(f"gate{r}", [P, T - OWN * P], F32) for r in range(2)]
+        gate_col = [[held(f"gate_col{b}_{r}", [P, 1], F32) for r in range(2)] for b in range(OWN)]
         for r in range(2):
-            nc.sync.dma_start(gate_t[r][:, SPARE * P :], gate[r])
+            nc.sync.dma_start(gate_t[r][:], gate[r, :, OWN * P :])
+        for r in range(2):
+            for b in range(OWN):
+                nc.sync.dma_start(gate_col[b][r][:], gate[r, 0, b * P : (b + 1) * P].rearrange("(p o) -> p o", o=1))
 
         w3 = held("w3", [P, H], I32)
         w1 = held("w1", [P, H], I32)
@@ -153,36 +158,39 @@ def tile_moe_sup_glu_relu_kernel(
 
         chunks = S // CHUNK
         y = [held(f"y{j}", [P, S], F32) for j in range(4)]
-        woven = {}
         codes = {}
         planes = {}
-        pairs = held("pairs", [P, (chunks + LAG) * CHUNK], U32)
-        pair_rows = pairs[:].rearrange("p (r s) -> p r s", s=CHUNK)
+        pairs = {}
+        woven = {}
+        for q in (3, 2):
+            both = held(f"woven_quarter{q}", [P, 8 * CHUNK], BF16)
+            woven[2 * q], woven[2 * q + 1] = both[:, : 4 * CHUNK], both[:, 4 * CHUNK :]
+            woven[2 * q, 2 * q + 1] = both[:]
 
-        def slots(s0, n):
-            return offs_t[:, s0 // 16 : (s0 + n) // 16]
+        def gather(c, u):
+            if c not in pairs:
+                pairs[c] = held(f"pairs{c}", [P, 2 * CHUNK], U32, tag=f"pairs{c if c >= chunks - EARLY else 4 + 2 * (c % 2)}")
+            view = "p (s u) -> p u s" if c == 0 else "p (u s) -> p u s"
+            nc.vector.tensor_copy(
+                pairs[c][:].rearrange(view, u=2)[:, u, :],
+                h[u][:].bitcast(U32).indirect(offs_t[:, c * CHUNK // 16 : (c + 1) * CHUNK // 16]),
+            )
 
-        def gather(c):
-            lst = slots(c * CHUNK, CHUNK)
-            if c == 0:
-                both = pairs[:, (2 + LAG) * CHUNK : (4 + LAG) * CHUNK]
-                woven[c] = both.bitcast(BF16)
-                for u in range(2):
-                    nc.vector.tensor_copy(
-                        both.rearrange("p (s u) -> p s u", u=2)[:, :, u], h[u][:].bitcast(U32).indirect(lst)
-                    )
-            else:
+        def weave(c, copy):
+            if c not in woven:
                 woven[c] = held(f"woven{c}", [P, 4 * CHUNK], BF16)[:]
-                nc.vector.tensor_copy(pair_rows[:, c + LAG, :], h[1][:].bitcast(U32).indirect(lst))
-                nc.scalar.copy(
-                    woven[c].bitcast(U32).rearrange("p (s u) -> p s u", u=2),
-                    pair_rows[:, c : c + LAG + 1 : LAG, :].rearrange("p u s -> p s u"),
-                )
+            copy(
+                woven[c].bitcast(U32).rearrange("p (s u) -> p s u", u=2),
+                pairs[c][:].rearrange("p (u s) -> p s u", u=2),
+            )
 
-        def quantise(c):
-            codes[c] = held(f"codes{c}", [P, CHUNK], U32)
-            planes[c] = held(f"planes{c}", [P, CHUNK], U8)
-            nc.vector.quantize_mx(out=codes[c][:].bitcast(FP8X4), scales=planes[c][:], in_=woven[c])
+        def quantise(c0, n, values):
+            words = held(f"codes{c0}", [P, n * CHUNK], U32)
+            plane = held(f"planes{c0}", [P, n * CHUNK], U8)
+            nc.vector.quantize_mx(out=words[:].bitcast(FP8X4), scales=plane[:], in_=values)
+            for i in range(n):
+                codes[c0 + i] = words[:, i * CHUNK : (i + 1) * CHUNK]
+                planes[c0 + i] = plane[:, i * CHUNK : (i + 1) * CHUNK]
 
         def second_product(j, s0, n, which):
             acc = bank(which)
@@ -201,27 +209,28 @@ def tile_moe_sup_glu_relu_kernel(
                 )
             return y[j][:, s0 : s0 + n], acc[:, :n]
 
-        for c0, c1 in ((5, 8), (3, 5), (1, 3)):
-            s0, n = c0 * CHUNK, (c1 - c0) * CHUNK
-            nc.vector.tensor_copy(pairs[:, s0 : s0 + n], h[0][:].bitcast(U32).indirect(slots(s0, n)))
-        for c in range(chunks - 1, 0, -1):
-            gather(c)
-            if c + 2 < chunks:
-                quantise(c + 2)
-        quantise(2)
-        gather(0)
-        for q in (3, 2, 1):
-            nc.scalar.copy(*second_product(0, q * BANK, BANK, 7 - q))
-        by_vector = [second_product(1, q * BANK, BANK, 3 - q) for q in (3, 2)]
-        quantise(1)
-        quantise(0)
-        nc.scalar.copy(*second_product(0, CHUNK, CHUNK, 7))
-        nc.scalar.copy(*second_product(0, 0, CHUNK, 2))
-        for copy_args in by_vector:
-            nc.vector.tensor_copy(*copy_args)
-        rest = [(1, 1), (1, 0)] + [(j, q) for j in (2, 3) for q in (3, 2, 1, 0)]
-        for (j, q), which in zip(rest, (3, 4, 5, 6, 7, 2, 3, 4, 0, 1)):
-            nc.scalar.copy(*second_product(j, q * BANK, BANK, which))
+        early = range(chunks - 1, chunks - 1 - EARLY, -1)
+        for c in early:
+            gather(c, 0)
+        for c in early:
+            gather(c, 1)
+            weave(c, nc.scalar.copy)
+        quantise(6, 2, woven[6, 7])
+        for c in (3, 2, 1, 0):
+            gather(c, 0)
+            gather(c, 1)
+            if c:
+                weave(c, nc.gpsimd.tensor_copy)
+            if c == 3:
+                quantise(4, 2, woven[4, 5])
+            else:
+                quantise(c + 1, 1, woven[c + 1])
+        quantise(0, 1, pairs[0][:].bitcast(BF16))
+        units = [(j, q * BANK, BANK) for q in (3, 2, 1) for j in range(4)]
+        units += [(0, CHUNK, CHUNK), (0, 0, CHUNK)] + [(j, 0, BANK) for j in (1, 2, 3)]
+        for k, (j, s0, n) in enumerate(units):
+            copy = nc.vector.tensor_copy if n == CHUNK else nc.scalar.copy
+            copy(*second_product(j, s0, n, (0, 1, 4, 5, 2, 3, 6, 7)[k % 8]))
 
         rounded = held("rounded", [P, 4 * T], BF16)
         out_rows = out_0.rearrange("(p t) w -> p t w", t=4)
@@ -231,32 +240,21 @@ def tile_moe_sup_glu_relu_kernel(
         backs = {}
         results = {}
 
-        def combine(b, n):
-            tok = b * P
-            if b == 0:
-                terms = [[held(f"term{j}_{r}", [P, n], F32)[:] for r in range(2)] for j in range(3)]
-                terms.append([g[:, :n] for g in gate_t])
-            else:
-                places = [4 * (b % 2) + j for j in range(3)] + [3 if b % 2 and b < last else 7]
-                terms = [[g[:, P * place : P * (place + 1)] for g in gate_t] for place in places]
-            for j in range(4):
-                width = P if j == 3 else n
-                for o in range(0, n, width):
-                    g0 = SPARE * P + tok + o
-                    for r in range(2):
-                        nc.vector.tensor_tensor(
-                            terms[j][r][:, o : o + width],
-                            y[j][:].indirect(pos_t[r][:, (tok + o) // 16 : (tok + o + width) // 16]),
-                            gate_t[r][:, g0 : g0 + width],
-                            MULT,
-                        )
-            return terms
+        def lookup(j, r, b, n=1):
+            return y[j][:].indirect(pos_t[r][:, b * P // 16 : (b + n) * P // 16])
 
-        def turn_rows(turned, terms, o, tiles):
+        def new_terms(b):
+            return [held(f"terms{b}_{r}", [P, 4, P], F32, tag=f"terms{b % 2}_{r}") for r in range(2)]
+
+        def combine(b, terms, j):
+            for r in range(2):
+                nc.vector.tensor_tensor(terms[r][:, j, :], lookup(j, r, b), gate_t[r][:, (b - OWN) * P : (b - OWN + 1) * P], MULT)
+
+        def turn_rows(turned, terms, tiles):
             for j in range(*tiles):
                 for r in range(2):
                     nc.tensor.matmul(
-                        turned[:, P * j : P * (j + 1)], terms[j][r][:, o : o + P], ident[:],
+                        turned[:, P * j : P * (j + 1)], terms[r][:, j, :], ident[:],
                         is_transpose=True, start=(r == 0), stop=(r == 1),
                     )
 
@@ -266,10 +264,14 @@ def tile_moe_sup_glu_relu_kernel(
                 turned[:, P * tiles[0] : P * tiles[1]].rearrange("p (m t) -> p t m", t=4),
             )
 
-        def turn_back(b, dealt):
-            backs[b] = bank((2, 3, 4, 0, 1)[b % 5])
+        def turn_back(b, *dealts):
+            backs[b] = bank((7, 0, 3, 6, 3, 6, 7)[b])
             for t in range(4):
-                nc.tensor.transpose(backs[b][:, P * t : P * (t + 1)], dealt[:, t, :], ident[:])
+                for r, dealt in enumerate(dealts):
+                    nc.tensor.matmul(
+                        backs[b][:, P * t : P * (t + 1)], dealt[:, t, :], ident[:],
+                        is_transpose=True, start=(r == 0), stop=(r == len(dealts) - 1),
+                    )
 
         def store(b):
             results[b] = held(f"result{b}", [P, 4, P], F32)
@@ -277,48 +279,87 @@ def tile_moe_sup_glu_relu_kernel(
             nc.sync.dma_start(out_rows[:, :, b * P : (b + 1) * P], results[b][:])
 
         def finish(b):
-            nc.scalar.copy(
-                rounded[:, 4 * P * b : 4 * P * (b + 1)].rearrange("p (w t) -> p w t", t=4),
-                backs[b][:].rearrange("p (t w) -> p w t", t=4),
-            )
+            cols = slice(4 * P * b, 4 * P * (b + 1))
+            if b in ROUNDED_BY_SCALAR:
+                nc.scalar.copy(
+                    rounded[:, cols].rearrange("p (w t) -> p w t", t=4),
+                    backs[b][:].rearrange("p (t w) -> p w t", t=4),
+                )
             store(b)
+            if b not in ROUNDED_BY_SCALAR:
+                nc.vector.tensor_copy(
+                    rounded[:, cols].rearrange("p (c i t) -> p c t i", t=4, i=4),
+                    results[b][:].rearrange("p t (c i) -> p c t i", i=4),
+                )
 
+        scaled = [[held(f"scaled{b}_{r}", [P, 4, P], F32) for r in range(2)] for b in range(OWN)]
+
+        def own_choice(r):
+            picked = held(f"picked{r}", [P, 4, OWN * P], F32)
+            turned = [bank(which) for which in (5, 2)]
+            for j in range(4):
+                nc.scalar.activation(picked[:, j, :], lookup(j, r, 0, OWN), COPY)
+                for b in range(OWN):
+                    nc.tensor.transpose(turned[b][:, P * j : P * (j + 1)], picked[:, j, b * P : (b + 1) * P], ident[:])
+            for b in range(OWN):
+                nc.scalar.activation(
+                    scaled[b][r][:], turned[b][:].rearrange("p (m t) -> p t m", t=4), COPY, scale=gate_col[b][r][:]
+                )
+
+        own_choice(0)
         halves = ((0, 2), (2, 4))
-        terms = combine(0, HEAD * P)
-        dealts = [ring.tile([P, 4, P], F32, name="dealt") for b in range(HEAD)]
-        turneds = [bank(5 + b) for b in range(HEAD)]
+        head = (OWN, OWN + 1)
+        terms = {b: new_terms(b) for b in head}
+        dealts = {b: ring.tile([P, 4, P], F32, name="dealt") for b in head}
+        turneds = {b: bank(which) for b, which in zip(head, (1, 4))}
         for tiles in halves:
-            for b in range(HEAD):
-                turn_rows(turneds[b], terms, b * P, tiles)
+            for j in range(*tiles):
+                for b in head:
+                    combine(b, terms[b], j)
+            for b in head:
+                turn_rows(turneds[b], terms[b], tiles)
                 deal_rows(dealts[b], turneds[b], tiles)
                 if tiles == halves[1]:
                     turn_back(b, dealts[b])
-                    if b:
-                        finish(b - 1)
-        for b in range(HEAD, last):
-            terms = combine(b, P)
+        own_choice(1)
+        finish(head[0])
+        for b in range(OWN):
+            turn_back(b, *scaled[b])
+        for b in range(head[-1] + 1, last):
+            terms = new_terms(b)
+            for j in range(4):
+                combine(b, terms, j)
             dealt = ring.tile([P, 4, P], F32, name="dealt")
-            for which, tiles in zip((5, 6), halves):
+            for which, tiles in zip((1, 4), halves):
                 turned = bank(which)
-                turn_rows(turned, terms, 0, tiles)
+                turn_rows(turned, terms, tiles)
                 deal_rows(dealt, turned, tiles)
+            if b == head[-1] + 1:
+                finish(b - 1)
+                finish(0)
             turn_back(b, dealt)
-            finish(b - 1)
+            if b == head[-1] + 1:
+                finish(1)
+            else:
+                finish(b - 1)
 
-        store(last - 1)
+        late = last - 1
+        store(late)
 
-        terms = combine(last, P)
+        terms = new_terms(last)
+        for j in range(4):
+            combine(last, terms, j)
         tok = last * P
         dealt_pairs = held("dealt_pairs", [P, 2, P, 2], BF16)
-        for which, tiles in zip((5, 6), ((0, 3), (3, 4))):
+        for which, tiles in zip((1, 4), ((0, 3), (3, 4))):
             turned = bank(which)
-            turn_rows(turned, terms, 0, tiles)
+            turn_rows(turned, terms, tiles)
             nc.scalar.copy(
                 dealt_pairs[:, :, 32 * tiles[0] : 32 * tiles[1], :],
                 turned[:, P * tiles[0] : P * tiles[1]].rearrange("p (m u e) -> p u m e", u=2, e=2),
             )
         pair_words = dealt_pairs[:].rearrange("p u m e -> p (u m e)").bitcast(F32)
-        back = bank(7)
+        back = bank(0)
         for u in range(2):
             nc.tensor.transpose(back[:, P * u : P * (u + 1)], pair_words[:, P * u : P * (u + 1)], ident[:])
 
@@ -342,8 +383,7 @@ def tile_moe_sup_glu_relu_kernel(
         )
         result_last = held("result_last", [P, 4, P], F32)
         nc.vector.tensor_tensor(
-            result_last[:].rearrange("p j w -> p (j w)"),
-            gate_t[0][:, 4 * P : 8 * P], gate_t[1][:, 4 * P : 8 * P], ADD,
+            result_last[:], terms[0][:], terms[1][:], ADD,
         )
         nc.sync.dma_start(out_0.rearrange("(j p) w -> p j w", j=4)[:, :, tok:], result_last[:])
         nc.scalar.copy(

@@ -258,11 +258,14 @@ def tile_moe_sup_glu_relu_kernel(
                         is_transpose=True, start=(r == 0), stop=(r == 1),
                     )
 
-        def deal_rows(dealt, turned, tiles):
-            nc.scalar.copy(
-                dealt[:, :, 32 * tiles[0] : 32 * tiles[1]],
-                turned[:, P * tiles[0] : P * tiles[1]].rearrange("p (m t) -> p t m", t=4),
+        def dealing(dealt, turned, tiles):
+            return (
+                dealt[:, :, 32 * tiles[0] : 32 * tiles[1]].rearrange("p t (c i) -> p c t i", i=4),
+                turned[:, P * tiles[0] : P * tiles[1]].rearrange("p (c i t) -> p c t i", t=4, i=4),
             )
+
+        def deal_rows(dealt, turned, tiles):
+            nc.scalar.copy(*dealing(dealt, turned, tiles))
 
         def turn_back(b, *dealts):
             backs[b] = bank((7, 0, 3, 6, 3, 6, 7)[b])
@@ -302,9 +305,7 @@ def tile_moe_sup_glu_relu_kernel(
                 for b in range(OWN):
                     nc.tensor.transpose(turned[b][:, P * j : P * (j + 1)], picked[:, j, b * P : (b + 1) * P], ident[:])
             for b in range(OWN):
-                nc.scalar.activation(
-                    scaled[b][r][:], turned[b][:].rearrange("p (m t) -> p t m", t=4), COPY, scale=gate_col[b][r][:]
-                )
+                nc.scalar.activation(*dealing(scaled[b][r], turned[b], (0, 4)), COPY, scale=gate_col[b][r][:])
 
         own_choice(0)
         halves = ((0, 2), (2, 4))

@@ -28,7 +28,8 @@ CHUNK = 256
 GPSIMD_STEPS = (4, 5)
 EARLY = 4
 OWN = 2
-ROUNDED_BY_SCALAR = (3, 4)
+LONG_ROAD = (4, 5)
+BACK_BANKS = (7, 0, 3, 6, 3, 6, 7, 0)
 COPY = mybir.ActivationFunctionType.Copy
 
 
@@ -268,7 +269,7 @@ def tile_moe_sup_glu_relu_kernel(
             nc.scalar.copy(*dealing(dealt, turned, tiles))
 
         def turn_back(b, *dealts):
-            backs[b] = bank((7, 0, 3, 6, 3, 6, 7)[b])
+            backs[b] = bank(BACK_BANKS[b])
             for t in range(4):
                 for r, dealt in enumerate(dealts):
                     nc.tensor.matmul(
@@ -282,18 +283,34 @@ def tile_moe_sup_glu_relu_kernel(
             nc.sync.dma_start(out_rows[:, :, b * P : (b + 1) * P], results[b][:])
 
         def finish(b):
-            cols = slice(4 * P * b, 4 * P * (b + 1))
-            if b in ROUNDED_BY_SCALAR:
-                nc.scalar.copy(
-                    rounded[:, cols].rearrange("p (w t) -> p w t", t=4),
-                    backs[b][:].rearrange("p (t w) -> p w t", t=4),
-                )
+            nc.scalar.copy(
+                rounded[:, 4 * P * b : 4 * P * (b + 1)].rearrange("p (w t) -> p w t", t=4),
+                backs[b][:].rearrange("p (t w) -> p w t", t=4),
+            )
             store(b)
-            if b not in ROUNDED_BY_SCALAR:
-                nc.vector.tensor_copy(
-                    rounded[:, cols].rearrange("p (c i t) -> p c t i", t=4, i=4),
-                    results[b][:].rearrange("p t (c i) -> p c t i", i=4),
-                )
+
+        def deal_pairs(pairs_out, turned, tiles):
+            nc.scalar.copy(
+                pairs_out[:, :, 32 * tiles[0] : 32 * tiles[1], :],
+                turned[:, P * tiles[0] : P * tiles[1]].rearrange("p (m u e) -> p u m e", u=2, e=2),
+            )
+
+        def turn_pairs_back(b, pairs_out):
+            backs[b] = bank(BACK_BANKS[b])
+            words = pairs_out[:].rearrange("p u m e -> p (u m e)").bitcast(F32)
+            for u in range(2):
+                nc.tensor.transpose(backs[b][:, P * u : P * (u + 1)], words[:, P * u : P * (u + 1)], ident[:])
+
+        def weave_pairs(b):
+            nc.scalar.copy(
+                rounded[:, 4 * P * b : 4 * P * (b + 1)].bitcast(F32).rearrange("p (w u) -> p w u", u=2),
+                backs[b][:, : 2 * P].rearrange("p (u w) -> p w u", u=2),
+            )
+
+        def add_and_store(b, terms, tag=""):
+            total = held(f"total{b}", [P, 4, P], F32, tag=tag)
+            nc.vector.tensor_tensor(total[:], terms[0][:], terms[1][:], ADD)
+            nc.sync.dma_start(out_0.rearrange("(j p) w -> p j w", j=4)[:, :, b * P : (b + 1) * P], total[:])
 
         scaled = [[held(f"scaled{b}_{r}", [P, 4, P], F32) for r in range(2)] for b in range(OWN)]
 
@@ -311,7 +328,7 @@ def tile_moe_sup_glu_relu_kernel(
         halves = ((0, 2), (2, 4))
         head = (OWN, OWN + 1)
         terms = {b: new_terms(b) for b in head}
-        dealts = {b: ring.tile([P, 4, P], F32, name="dealt") for b in head}
+        dealts = {b: held(f"dealt_pairs{b}", [P, 2, P, 2], BF16) for b in head}
         turneds = {b: bank(which) for b, which in zip(head, (1, 4))}
         for tiles in halves:
             for j in range(*tiles):
@@ -319,14 +336,16 @@ def tile_moe_sup_glu_relu_kernel(
                     combine(b, terms[b], j)
             for b in head:
                 turn_rows(turneds[b], terms[b], tiles)
-                deal_rows(dealts[b], turneds[b], tiles)
+                deal_pairs(dealts[b], turneds[b], tiles)
                 if tiles == halves[1]:
-                    turn_back(b, dealts[b])
+                    turn_pairs_back(b, dealts[b])
+        for b in head:
+            add_and_store(b, terms[b])
+            weave_pairs(b)
         own_choice(1)
-        finish(head[0])
         for b in range(OWN):
             turn_back(b, *scaled[b])
-        for b in range(head[-1] + 1, last):
+        for b in LONG_ROAD:
             terms = new_terms(b)
             for j in range(4):
                 combine(b, terms, j)
@@ -335,34 +354,26 @@ def tile_moe_sup_glu_relu_kernel(
                 turned = bank(which)
                 turn_rows(turned, terms, tiles)
                 deal_rows(dealt, turned, tiles)
-            if b == head[-1] + 1:
-                finish(b - 1)
-                finish(0)
             turn_back(b, dealt)
-            if b == head[-1] + 1:
-                finish(1)
+            if b == LONG_ROAD[0]:
+                for own in range(OWN):
+                    finish(own)
             else:
                 finish(b - 1)
-
-        late = last - 1
-        store(late)
-
-        terms = new_terms(last)
-        for j in range(4):
-            combine(last, terms, j)
-        tok = last * P
-        dealt_pairs = held("dealt_pairs", [P, 2, P, 2], BF16)
-        for which, tiles in zip((1, 4), ((0, 3), (3, 4))):
-            turned = bank(which)
-            turn_rows(turned, terms, tiles)
-            nc.scalar.copy(
-                dealt_pairs[:, :, 32 * tiles[0] : 32 * tiles[1], :],
-                turned[:, P * tiles[0] : P * tiles[1]].rearrange("p (m u e) -> p u m e", u=2, e=2),
-            )
-        pair_words = dealt_pairs[:].rearrange("p u m e -> p (u m e)").bitcast(F32)
-        back = bank(0)
-        for u in range(2):
-            nc.tensor.transpose(back[:, P * u : P * (u + 1)], pair_words[:, P * u : P * (u + 1)], ident[:])
+        terms = {}
+        for b, parts in ((last - 1, halves), (last, ((0, 3), (3, 4)))):
+            terms[b] = new_terms(b)
+            for j in range(4):
+                combine(b, terms[b], j)
+            dealt = held(f"dealt_pairs{b}", [P, 2, P, 2], BF16)
+            for which, tiles in zip((1, 4), parts):
+                turned = bank(which)
+                turn_rows(turned, terms[b], tiles)
+                deal_pairs(dealt, turned, tiles)
+            turn_pairs_back(b, dealt)
+            if b < last:
+                finish(b - 1)
+                weave_pairs(b)
 
         out_codes = held("out_codes", [P, T], U32, tag="y3")
         out_plane = held("out_plane", [P, T], U8, tag="y2")
@@ -377,20 +388,10 @@ def tile_moe_sup_glu_relu_kernel(
             cols = slice(parts[0][0] * P, parts[-1][1] * P)
             nc.sync.dma_start(out_words[:, cols], out_codes[:, cols].bitcast(I32))
 
+        add_and_store(last - 1, terms[last - 1], tag="gate0")
         planes_of(((0, 4),))
-        nc.vector.tensor_copy(
-            rounded[:, 4 * P * (last - 1) : 4 * P * last].rearrange("p (c i t) -> p c t i", t=4, i=4),
-            results[last - 1][:].rearrange("p t (c i) -> p c t i", i=4),
-        )
-        result_last = held("result_last", [P, 4, P], F32)
-        nc.vector.tensor_tensor(
-            result_last[:], terms[0][:], terms[1][:], ADD,
-        )
-        nc.sync.dma_start(out_0.rearrange("(j p) w -> p j w", j=4)[:, :, tok:], result_last[:])
-        nc.scalar.copy(
-            rounded[:, 4 * tok :].bitcast(F32).rearrange("p (w u) -> p w u", u=2),
-            back[:, : 2 * P].rearrange("p (u w) -> p w u", u=2),
-        )
+        add_and_store(last, terms[last])
+        weave_pairs(last)
         planes_of(((4, 6), (6, 7)))
         planes_of(((7, 8),))
         scale_rows = out_2[0].bitcast(I32).rearrange("(q r) n -> r q n", r=4)

@@ -17,20 +17,20 @@ FP8X4 = mybir.dt.float8_e4m3fn_x4
 FP4X4 = mybir.dt.float4_e2m1fn_x4
 MULT = mybir.AluOpType.mult
 ADD = mybir.AluOpType.add
-RELU = mybir.ActivationFunctionType.Relu
 MAX = mybir.AluOpType.max
+RELU = mybir.ActivationFunctionType.Relu
+COPY = mybir.ActivationFunctionType.Copy
 
 P = 128
 BANK = 512
 STEP = BANK // 2
 AHEAD = 2
 CHUNK = 256
-GPSIMD_STEPS = (4, 5)
-EARLY = 4
-OWN = 2
-LONG_ROAD = (4, 5)
-BACK_BANKS = (7, 0, 3, 6, 3, 6, 7, 0)
-COPY = mybir.ActivationFunctionType.Copy
+EARLY, LATE = 1, 0
+GPSIMD_STEPS = 3
+SCALAR_WEAVES = 5
+OWN = 3
+ROUND = 3
 
 
 def tile_moe_sup_glu_relu_kernel(
@@ -40,7 +40,6 @@ def tile_moe_sup_glu_relu_kernel(
     nc = tc.nc
     with ExitStack() as ctx:
         keep = ctx.enter_context(tc.tile_pool(name="keep", bufs=1))
-        ring = ctx.enter_context(tc.tile_pool(name="ring", bufs=4))
         psum = ctx.enter_context(tc.psum_pool(name="psum", bufs=1))
 
         def held(name, shape, dtype, tag=""):
@@ -68,7 +67,6 @@ def tile_moe_sup_glu_relu_kernel(
         w1_raw = held("w1_raw", [P, H], I32)
         xw = [held(f"xw{a}", [P, T // 2], I32) for a in range(2)]
         xs_rows = x_scales[0].bitcast(I32).rearrange("(q r) n -> r q n", r=4)
-        w1s_rows = w1_scales[0].bitcast(I32).rearrange("(q r) n -> r q n", r=4)
         x_all = x_words[0].rearrange("p t d -> p (t d)").bitcast(I32)
         load_scale_rows(xs, xs_rows, (0, 1))
         load_scale_rows(w3s_raw, w3_scales[0].bitcast(I32).rearrange("(q r) n -> r q n", r=4))
@@ -76,12 +74,12 @@ def tile_moe_sup_glu_relu_kernel(
         nc.sync.dma_start(xw[0][:], x_all[:, : T // 2])
         load_scale_rows(xs, xs_rows, (2, 3))
         nc.sync.dma_start(w1_raw[:], w1_words[0].rearrange("p i d -> p (i d)").bitcast(I32))
-        load_scale_rows(w1s_raw, w1s_rows)
+        load_scale_rows(w1s_raw, w1_scales[0].bitcast(I32).rearrange("(q r) n -> r q n", r=4))
         nc.sync.dma_start(xw[1][:], x_all[:, T // 2 :])
         offs_t = held("offs_t", [P, S // 16], U16)
         nc.sync.dma_start(offs_t[:], offs)
         w2w = [held(f"w2w{a}", [P, 4 * 2 * N], U8) for a in range(4)]
-        for a in reversed(range(4)):
+        for a in range(4):
             nc.sync.dma_start(
                 w2w[a][:].bitcast(I32).rearrange("p (e c) -> p e c", e=4),
                 w2_words[4 * a : 4 * a + 4].bitcast(I32).rearrange("e s p c -> p (e s) c"),
@@ -103,7 +101,7 @@ def tile_moe_sup_glu_relu_kernel(
         w3s = held("w3s", [P, H], U8)
         w1s = held("w1s", [P, H], U8)
         for operand in (((w3, w3_raw, 4), (w3s, w3s_raw, 16)), ((w1, w1_raw, 4), (w1s, w1s_raw, 16))):
-            for u in range(2):
+            for u in (EARLY, LATE):
                 for dst, src, run in operand:
                     nc.vector.tensor_copy(
                         dst[:].rearrange("p (t c i) -> p c t i", t=4, i=run)[:, :, 2 * u : 2 * u + 2, :],
@@ -126,10 +124,10 @@ def tile_moe_sup_glu_relu_kernel(
                 )
             return acc[:].rearrange("p (e t) -> p t e", e=2)
 
-        steps = [(u, (tok + u * T // 2) % T) for u in range(2) for tok in range(0, T, STEP)]
+        steps = [(EARLY, tok) for tok in range(0, T, STEP)] + [(LATE, (tok + T // 2) % T) for tok in range(0, T, STEP)]
+        half = len(steps) // 2
+        step_banks = [(i, half + i) for i in range(half)] + [(i, i + 1) for i in (0, 4, 2, 6)]
         a3_sb = [held(f"a3_sb{i}", [P, STEP, 2], F32) for i in range(len(steps))]
-
-        step_banks = [(i, 4 + i) for i in range(4)] + [(i, i + 1) for i in (0, 4, 2, 6)]
 
         def linear_half(i):
             nc.scalar.copy(a3_sb[i][:], first_product(w3, w3s, *steps[i], bank(step_banks[i][0])))
@@ -138,7 +136,7 @@ def tile_moe_sup_glu_relu_kernel(
             u, tok = steps[i]
             a1 = first_product(w1, w1s, u, tok, bank(step_banks[i][1]))
             out = h[u][:, 2 * tok : 2 * (tok + STEP)].rearrange("p (t e) -> p t e", e=2)
-            if i in GPSIMD_STEPS:
+            if half <= i < half + GPSIMD_STEPS:
                 a1_sb = held(f"a1_sb{i}", [P, STEP, 2], F32)
                 nc.scalar.activation(a1_sb[:], a1, RELU)
                 nc.gpsimd.tensor_tensor(out, a1_sb[:], a3_sb[i][:], MULT)
@@ -154,46 +152,39 @@ def tile_moe_sup_glu_relu_kernel(
                 linear_half(i)
             gated_half(i)
 
-        ident = held("ident", [P, P], F32, tag=f"a1_sb{GPSIMD_STEPS[-1]}")
+        ident = held("ident", [P, P], F32, tag=f"a1_sb{half + GPSIMD_STEPS - 1}")
         make_identity(nc, ident[:])
 
         chunks = S // CHUNK
+        places = [(0, 1), (3, 4), (9, 10), (1, 2), (4, 5), (4, 7), (5, 6), (7, 8)]
+        pairs = held("pairs", [P, 11 * CHUNK], U32)
         y = [held(f"y{j}", [P, S], F32) for j in range(4)]
+        woven = {}
         codes = {}
         planes = {}
-        pairs = {}
-        woven = {}
-        for q in (3, 2):
-            both = held(f"woven_quarter{q}", [P, 8 * CHUNK], BF16)
-            woven[2 * q], woven[2 * q + 1] = both[:, : 4 * CHUNK], both[:, 4 * CHUNK :]
-            woven[2 * q, 2 * q + 1] = both[:]
 
-        def gather(c, u):
-            if c not in pairs:
-                pairs[c] = held(f"pairs{c}", [P, 2 * CHUNK], U32, tag=f"pairs{c if c >= chunks - EARLY else 4 + 2 * (c % 2)}")
-            view = "p (s u) -> p u s" if c == 0 else "p (u s) -> p u s"
+        def gather(u, c):
+            place = places[c][u]
             nc.vector.tensor_copy(
-                pairs[c][:].rearrange(view, u=2)[:, u, :],
+                pairs[:, place * CHUNK : (place + 1) * CHUNK],
                 h[u][:].bitcast(U32).indirect(offs_t[:, c * CHUNK // 16 : (c + 1) * CHUNK // 16]),
             )
 
-        def weave(c, copy):
-            if c not in woven:
-                woven[c] = held(f"woven{c}", [P, 4 * CHUNK], BF16)[:]
+        def weave(c):
+            woven[c] = held(f"woven{c}", [P, 4 * CHUNK], BF16)
+            late, early = places[c]
+            copy = nc.scalar.copy if c < SCALAR_WEAVES else nc.vector.tensor_copy
             copy(
-                woven[c].bitcast(U32).rearrange("p (s u) -> p s u", u=2),
-                pairs[c][:].rearrange("p (u s) -> p s u", u=2),
+                woven[c][:].bitcast(U32).rearrange("p (s u) -> p s u", u=2),
+                pairs[:].rearrange("p (k s) -> p s k", s=CHUNK)[:, :, late : early + 1 : early - late],
             )
 
-        def quantise(c0, n, values):
-            words = held(f"codes{c0}", [P, n * CHUNK], U32)
-            plane = held(f"planes{c0}", [P, n * CHUNK], U8)
-            nc.vector.quantize_mx(out=words[:].bitcast(FP8X4), scales=plane[:], in_=values)
-            for i in range(n):
-                codes[c0 + i] = words[:, i * CHUNK : (i + 1) * CHUNK]
-                planes[c0 + i] = plane[:, i * CHUNK : (i + 1) * CHUNK]
+        def quantise(c):
+            codes[c] = held(f"codes{c}", [P, CHUNK], U32)
+            planes[c] = held(f"planes{c}", [P, CHUNK], U8)
+            nc.vector.quantize_mx(out=codes[c][:].bitcast(FP8X4), scales=planes[c][:], in_=woven[c][:])
 
-        def second_product(j, s0, n, which):
+        def second_product(j, s0, n, which, copy):
             acc = bank(which)
             for s in range(s0, s0 + n, C):
                 e = s // C
@@ -208,192 +199,188 @@ def tile_moe_sup_glu_relu_kernel(
                     start=True,
                     stop=True,
                 )
-            return y[j][:, s0 : s0 + n], acc[:, :n]
+            copy(y[j][:, s0 : s0 + n], acc[:, :n])
 
-        early = range(chunks - 1, chunks - 1 - EARLY, -1)
-        for c in early:
-            gather(c, 0)
-        for c in early:
-            gather(c, 1)
-            weave(c, nc.scalar.copy)
-        quantise(6, 2, woven[6, 7])
-        for c in (3, 2, 1, 0):
-            gather(c, 0)
-            gather(c, 1)
-            if c:
-                weave(c, nc.gpsimd.tensor_copy)
-            if c == 3:
-                quantise(4, 2, woven[4, 5])
-            else:
-                quantise(c + 1, 1, woven[c + 1])
-        quantise(0, 1, pairs[0][:].bitcast(BF16))
-        units = [(j, q * BANK, BANK) for q in (3, 2, 1) for j in range(4)]
-        units += [(0, CHUNK, CHUNK), (0, 0, CHUNK)] + [(j, 0, BANK) for j in (1, 2, 3)]
+        for c in range(chunks):
+            gather(EARLY, c)
+        for c in range(3):
+            gather(LATE, c)
+        for c in range(SCALAR_WEAVES):
+            weave(c)
+            if c + 3 < SCALAR_WEAVES:
+                gather(LATE, c + 3)
+            if c + 1 < SCALAR_WEAVES:
+                quantise(c)
+        gather(LATE, 5)
+        gather(LATE, 6)
+        weave(5)
+        quantise(4)
+        gather(LATE, 7)
+        weave(6)
+        quantise(5)
+        weave(7)
+        quantise(6)
+        quantise(7)
+
+        turn = (0, 1, 4, 5, 2, 3, 6, 7)
+        units = [(j, 0, BANK) for j in range(4)] + [(j, BANK, BANK) for j in range(3)]
+        units += [(0, 2 * BANK, BANK), (0, 6 * CHUNK, CHUNK), (0, 7 * CHUNK, CHUNK), (3, BANK, BANK)]
+        units += [(j, q * BANK, BANK) for j in (1, 2, 3) for q in (2, 3)]
         for k, (j, s0, n) in enumerate(units):
-            copy = nc.vector.tensor_copy if n == CHUNK else nc.scalar.copy
-            copy(*second_product(j, s0, n, (0, 1, 4, 5, 2, 3, 6, 7)[k % 8]))
+            second_product(j, s0, n, turn[k % 8], nc.vector.tensor_copy if n == CHUNK else nc.scalar.copy)
 
-        rounded = held("rounded", [P, 4 * T], BF16)
         out_rows = out_0.rearrange("(p t) w -> p t w", t=4)
+        out_tiles = out_0.rearrange("(j p) w -> p j w", j=4)
         out_words = out_1[0].rearrange("p t d -> p (t d)").bitcast(I32)
         blocks = T // P
         last = blocks - 1
-        backs = {}
-        results = {}
 
-        def lookup(j, r, b, n=1):
-            return y[j][:].indirect(pos_t[r][:, b * P // 16 : (b + n) * P // 16])
+        def lookup(j, r, t0, n):
+            return y[j][:].indirect(pos_t[r][:, t0 // 16 : (t0 + n) // 16])
 
-        def new_terms(b):
-            return [held(f"terms{b}_{r}", [P, 4, P], F32, tag=f"terms{b % 2}_{r}") for r in range(2)]
+        def gated(out, j, r, t0, n):
+            nc.vector.tensor_tensor(out, lookup(j, r, t0, n), gate_t[r][:, t0 - OWN * P : t0 - OWN * P + n], MULT)
 
-        def combine(b, terms, j):
-            for r in range(2):
-                nc.vector.tensor_tensor(terms[r][:, j, :], lookup(j, r, b), gate_t[r][:, (b - OWN) * P : (b - OWN + 1) * P], MULT)
-
-        def turn_rows(turned, terms, tiles):
-            for j in range(*tiles):
-                for r in range(2):
-                    nc.tensor.matmul(
-                        turned[:, P * j : P * (j + 1)], terms[r][:, j, :], ident[:],
-                        is_transpose=True, start=(r == 0), stop=(r == 1),
-                    )
-
-        def dealing(dealt, turned, tiles):
-            return (
-                dealt[:, :, 32 * tiles[0] : 32 * tiles[1]].rearrange("p t (c i) -> p c t i", i=4),
-                turned[:, P * tiles[0] : P * tiles[1]].rearrange("p (c i t) -> p c t i", t=4, i=4),
-            )
-
-        def deal_rows(dealt, turned, tiles):
-            nc.scalar.copy(*dealing(dealt, turned, tiles))
-
-        def turn_back(b, *dealts):
-            backs[b] = bank(BACK_BANKS[b])
-            for t in range(4):
-                for r, dealt in enumerate(dealts):
-                    nc.tensor.matmul(
-                        backs[b][:, P * t : P * (t + 1)], dealt[:, t, :], ident[:],
-                        is_transpose=True, start=(r == 0), stop=(r == len(dealts) - 1),
-                    )
-
-        def store(b):
-            results[b] = held(f"result{b}", [P, 4, P], F32)
-            nc.scalar.copy(results[b][:], backs[b][:].rearrange("p (t w) -> p t w", t=4))
-            nc.sync.dma_start(out_rows[:, :, b * P : (b + 1) * P], results[b][:])
-
-        def finish(b):
-            nc.scalar.copy(
-                rounded[:, 4 * P * b : 4 * P * (b + 1)].rearrange("p (w t) -> p w t", t=4),
-                backs[b][:].rearrange("p (t w) -> p w t", t=4),
-            )
-            store(b)
-
-        def deal_pairs(pairs_out, turned, tiles):
-            nc.scalar.copy(
-                pairs_out[:, :, 32 * tiles[0] : 32 * tiles[1], :],
-                turned[:, P * tiles[0] : P * tiles[1]].rearrange("p (m u e) -> p u m e", u=2, e=2),
-            )
-
-        def turn_pairs_back(b, pairs_out):
-            backs[b] = bank(BACK_BANKS[b])
-            words = pairs_out[:].rearrange("p u m e -> p (u m e)").bitcast(F32)
-            for u in range(2):
-                nc.tensor.transpose(backs[b][:, P * u : P * (u + 1)], words[:, P * u : P * (u + 1)], ident[:])
-
-        def weave_pairs(b):
-            nc.scalar.copy(
-                rounded[:, 4 * P * b : 4 * P * (b + 1)].bitcast(F32).rearrange("p (w u) -> p w u", u=2),
-                backs[b][:, : 2 * P].rearrange("p (u w) -> p w u", u=2),
-            )
-
-        def add_and_store(b, terms, tag=""):
-            total = held(f"total{b}", [P, 4, P], F32, tag=tag)
-            nc.vector.tensor_tensor(total[:], terms[0][:], terms[1][:], ADD)
-            nc.sync.dma_start(out_0.rearrange("(j p) w -> p j w", j=4)[:, :, b * P : (b + 1) * P], total[:])
+        first = OWN * P
+        width = ROUND * P
+        cut = width - P
+        for j in range(4):
+            terms = [held(f"round_terms{j}_{r}", [P, width], F32) for r in range(2)]
+            total = held(f"round_total{j}", [P, width], F32)
+            gated(terms[0][:], j, 0, first, width)
+            for t0, n in ((0, cut), (cut, P)):
+                gated(terms[1][:, t0 : t0 + n], j, 1, first + t0, n)
+            for t0, n in ((0, cut), (cut, P)):
+                nc.vector.tensor_tensor(total[:, t0 : t0 + n], terms[0][:, t0 : t0 + n], terms[1][:, t0 : t0 + n], ADD)
+            nc.sync.dma_start(out_tiles[:, j, first : first + width], total[:])
+        regrouped = held("regrouped", [P, 4, width], F32)
+        nc.sync.dma_start(regrouped[:], out_rows[:, :, first : first + width])
 
         scaled = [[held(f"scaled{b}_{r}", [P, 4, P], F32) for r in range(2)] for b in range(OWN)]
 
-        def own_choice(r):
-            picked = held(f"picked{r}", [P, 4, OWN * P], F32)
-            turned = [bank(which) for which in (5, 2)]
-            for j in range(4):
-                nc.scalar.activation(picked[:, j, :], lookup(j, r, 0, OWN), COPY)
-                for b in range(OWN):
-                    nc.tensor.transpose(turned[b][:, P * j : P * (j + 1)], picked[:, j, b * P : (b + 1) * P], ident[:])
-            for b in range(OWN):
-                nc.scalar.activation(*dealing(scaled[b][r], turned[b], (0, 4)), COPY, scale=gate_col[b][r][:])
+        def own_choice(r, b0, b1, banks, tag=""):
+            turned = {b: bank(which) for b, which in zip(range(b0, b1), banks)}
+            for j in (3, 0, 1, 2):
+                picked = held(f"picked{b0}_{r}_{j}", [P, (b1 - b0) * P], F32, tag=tag and f"{tag}_{j}")
+                nc.scalar.activation(picked[:], lookup(j, r, b0 * P, (b1 - b0) * P), COPY)
+                for b in range(b0, b1):
+                    nc.tensor.transpose(
+                        turned[b][:, P * j : P * (j + 1)], picked[:, (b - b0) * P : (b - b0 + 1) * P], ident[:]
+                    )
+            return turned
 
-        own_choice(0)
-        halves = ((0, 2), (2, 4))
-        head = (OWN, OWN + 1)
-        terms = {b: new_terms(b) for b in head}
-        dealts = {b: held(f"dealt_pairs{b}", [P, 2, P, 2], BF16) for b in head}
-        turneds = {b: bank(which) for b, which in zip(head, (1, 4))}
-        for tiles in halves:
-            for j in range(*tiles):
-                for b in head:
-                    combine(b, terms[b], j)
-            for b in head:
-                turn_rows(turneds[b], terms[b], tiles)
-                deal_pairs(dealts[b], turneds[b], tiles)
-                if tiles == halves[1]:
-                    turn_pairs_back(b, dealts[b])
-        for b in head:
-            add_and_store(b, terms[b])
-            weave_pairs(b)
-        own_choice(1)
-        for b in range(OWN):
-            turn_back(b, *scaled[b])
-        for b in LONG_ROAD:
-            terms = new_terms(b)
-            for j in range(4):
-                combine(b, terms, j)
-            dealt = ring.tile([P, 4, P], F32, name="dealt")
-            for which, tiles in zip((1, 4), halves):
-                turned = bank(which)
-                turn_rows(turned, terms, tiles)
-                deal_rows(dealt, turned, tiles)
-            turn_back(b, dealt)
-            if b == LONG_ROAD[0]:
-                for own in range(OWN):
-                    finish(own)
-            else:
-                finish(b - 1)
-        terms = {}
-        for b, parts in ((last - 1, halves), (last, ((0, 3), (3, 4)))):
-            terms[b] = new_terms(b)
-            for j in range(4):
-                combine(b, terms[b], j)
-            dealt = held(f"dealt_pairs{b}", [P, 2, P, 2], BF16)
-            for which, tiles in zip((1, 4), parts):
-                turned = bank(which)
-                turn_rows(turned, terms[b], tiles)
-                deal_pairs(dealt, turned, tiles)
-            turn_pairs_back(b, dealt)
-            if b < last:
-                finish(b - 1)
-                weave_pairs(b)
+        def own_deal(b, r, turned):
+            nc.scalar.activation(
+                scaled[b][r][:].rearrange("p t (c i) -> p c t i", i=4),
+                turned[:].rearrange("p (c i t) -> p c t i", t=4, i=4),
+                COPY, scale=gate_col[b][r][:],
+            )
 
-        out_codes = held("out_codes", [P, T], U32, tag="y3")
-        out_plane = held("out_plane", [P, T], U8, tag="y2")
+        results = [held(f"result{b}", [P, 4, P], F32) for b in range(OWN)]
 
-        def planes_of(parts):
-            for b0, b1 in parts:
-                cols = slice(b0 * P, b1 * P)
-                nc.vector.quantize_mx(
-                    out=out_codes[:, cols].bitcast(FP8X4), scales=out_plane[:, cols],
-                    in_=rounded[:, 4 * b0 * P : 4 * b1 * P],
-                )
-            cols = slice(parts[0][0] * P, parts[-1][1] * P)
+        def own_back(b, which):
+            back = bank(which)
+            for t in range(4):
+                for r in range(2):
+                    nc.tensor.matmul(
+                        back[:, P * t : P * (t + 1)], scaled[b][r][:, t, :], ident[:],
+                        is_transpose=True, start=(r == 0), stop=(r == 1),
+                    )
+            return back
+
+        def own_store(b, back):
+            nc.scalar.copy(results[b][:], back[:].rearrange("p (t w) -> p t w", t=4))
+            nc.sync.dma_start(out_rows[:, :, b * P : (b + 1) * P], results[b][:])
+
+        turned = [own_choice(r, 0, 2, turn[1 + 2 * r : 3 + 2 * r]) for r in range(2)]
+        for r in range(2):
+            for b in range(2):
+                own_deal(b, r, turned[r][b])
+        backs = [own_back(b, turn[1 + b]) for b in range(2)]
+        turned = [own_choice(0, 2, 3, turn[5:6], "picked0_1"), own_choice(1, 2, 3, turn[6:7], "picked0_1")]
+        for b in range(2):
+            own_store(b, backs[b])
+        for r in range(2):
+            own_deal(2, r, turned[r][2])
+        backs.append(own_back(2, turn[7]))
+
+        rounded = held("rounded", [P, 4 * T], BF16, tag="y0")
+        tail_terms = held("tail_terms", [P, 2, 2, 4, P], F32, tag="picked0_0_3")
+        tail_total = held("tail_total", [P, 4, 2 * P], F32)
+
+        def tail_gather(a, j, r):
+            gated(tail_terms[:, a, r, j, :], j, r, (last - 1 + a) * P, P)
+
+        def tail_add(a, j0, j1):
+            nc.vector.tensor_tensor(
+                tail_total[:, j0:j1, a * P : (a + 1) * P], tail_terms[:, a, 0, j0:j1, :], tail_terms[:, a, 1, j0:j1, :], ADD
+            )
+
+        def tail_turn(a, dealt, j0, j1, which):
+            turned = bank(which)
+            for j in range(j0, j1):
+                nc.tensor.transpose(turned[:, P * j : P * (j + 1)], tail_total[:, j, a * P : (a + 1) * P], ident[:])
+            nc.scalar.copy(
+                dealt[:, :, 32 * j0 : 32 * j1, :],
+                turned[:, P * j0 : P * j1].rearrange("p (m u e) -> p u m e", u=2, e=2),
+            )
+
+        def tail_back(a, dealt, which):
+            back = bank(which)
+            words = dealt[:].rearrange("p u m e -> p (u m e)").bitcast(F32)
+            for u in range(2):
+                nc.tensor.transpose(back[:, P * u : P * (u + 1)], words[:, P * u : P * (u + 1)], ident[:])
+            b = last - 1 + a
+            nc.scalar.copy(
+                rounded[:, 4 * P * b : 4 * P * (b + 1)].bitcast(F32).rearrange("p (w u) -> p w u", u=2),
+                back[:, : 2 * P].rearrange("p (u w) -> p w u", u=2),
+            )
+
+        for j in range(4):
+            for r in range(2):
+                tail_gather(0, j, r)
+        for r in range(2):
+            tail_gather(1, 0, r)
+        tail_add(0, 0, 4)
+        for j in (1, 2):
+            for r in range(2):
+                tail_gather(1, j, r)
+        tail_gather(1, 3, 0)
+        tail_add(1, 0, 3)
+        tail_gather(1, 3, 1)
+        tail_add(1, 3, 4)
+        nc.sync.dma_start(out_tiles[:, :, (last - 1) * P :], tail_total[:])
+        dealts = [held(f"dealt_pairs{a}", [P, 2, P, 2], BF16) for a in range(2)]
+        tail_turn(0, dealts[0], 0, 4, turn[1])
+        own_store(2, backs[2])
+        tail_turn(1, dealts[1], 0, 3, turn[2])
+        tail_turn(1, dealts[1], 3, 4, turn[5])
+        tail_back(0, dealts[0], turn[3])
+        tail_back(1, dealts[1], turn[4])
+
+        out_codes = held("out_codes", [P, T], U32)
+        out_plane = held("out_plane", [P, T], U8)
+
+        def round_rows(rows, t0, n):
+            nc.vector.tensor_copy(
+                rounded[:, 4 * t0 : 4 * (t0 + n)].rearrange("p (c i t) -> p c t i", t=4, i=4),
+                rows.rearrange("p t (c i) -> p c t i", i=4),
+            )
+
+        def planes_of(t0, n):
+            cols = slice(t0, t0 + n)
+            nc.vector.quantize_mx(
+                out=out_codes[:, cols].bitcast(FP8X4), scales=out_plane[:, cols], in_=rounded[:, 4 * t0 : 4 * (t0 + n)],
+            )
             nc.sync.dma_start(out_words[:, cols], out_codes[:, cols].bitcast(I32))
 
-        add_and_store(last - 1, terms[last - 1], tag="gate0")
-        planes_of(((0, 4),))
-        add_and_store(last, terms[last])
-        weave_pairs(last)
-        planes_of(((4, 6), (6, 7)))
-        planes_of(((7, 8),))
+        round_rows(regrouped[:], first, width)
+        round_rows(results[0][:], 0, P)
+        planes_of(first, width)
+        for b in range(1, OWN):
+            round_rows(results[b][:], b * P, P)
+        planes_of(0, OWN * P)
+        planes_of((last - 1) * P, 2 * P)
         scale_rows = out_2[0].bitcast(I32).rearrange("(q r) n -> r q n", r=4)
         for r in range(4):
             (nc.scalar if r < 3 else nc.sync).dma_start(scale_rows[r], out_plane[r:P:32, :].bitcast(I32))

@@ -155,9 +155,8 @@ def tile_moe_sup_glu_relu_kernel(
         ident = held("ident", [P, P], F32, tag=f"a1_sb{half + GPSIMD_STEPS - 1}")
         make_identity(nc, ident[:])
 
-        chunks = S // CHUNK
-        places = [(0, 1), (3, 4), (9, 10), (1, 2), (4, 5), (4, 7), (5, 6), (7, 8)]
-        pairs = held("pairs", [P, 11 * CHUNK], U32)
+        places = [(0, 1), (3, 4), (7, 8), (1, 2), (4, 5), (1, 2), (5, 6), (1, 2)]
+        pairs = held("pairs", [P, 9 * CHUNK], U32)
         y = [held(f"y{j}", [P, S], F32) for j in range(4)]
         woven = {}
         codes = {}
@@ -171,18 +170,18 @@ def tile_moe_sup_glu_relu_kernel(
             )
 
         def weave(c):
-            woven[c] = held(f"woven{c}", [P, 4 * CHUNK], BF16)
+            woven[c] = pairs[:, 3 * CHUNK : 5 * CHUNK] if c == 5 else held(f"woven{c}", [P, 2 * CHUNK], U32)[:]
             late, early = places[c]
             copy = nc.scalar.copy if c < SCALAR_WEAVES else nc.vector.tensor_copy
             copy(
-                woven[c][:].bitcast(U32).rearrange("p (s u) -> p s u", u=2),
+                woven[c].rearrange("p (s u) -> p s u", u=2),
                 pairs[:].rearrange("p (k s) -> p s k", s=CHUNK)[:, :, late : early + 1 : early - late],
             )
 
         def quantise(c):
             codes[c] = held(f"codes{c}", [P, CHUNK], U32)
             planes[c] = held(f"planes{c}", [P, CHUNK], U8)
-            nc.vector.quantize_mx(out=codes[c][:].bitcast(FP8X4), scales=planes[c][:], in_=woven[c][:])
+            nc.vector.quantize_mx(out=codes[c][:].bitcast(FP8X4), scales=planes[c][:], in_=woven[c].bitcast(BF16))
 
         def second_product(j, s0, n, which, copy):
             acc = bank(which)
@@ -201,7 +200,7 @@ def tile_moe_sup_glu_relu_kernel(
                 )
             copy(y[j][:, s0 : s0 + n], acc[:, :n])
 
-        for c in range(chunks):
+        for c in (0, 1, 2, 3, 4, 6):
             gather(EARLY, c)
         for c in range(3):
             gather(LATE, c)
@@ -211,23 +210,28 @@ def tile_moe_sup_glu_relu_kernel(
                 gather(LATE, c + 3)
             if c + 1 < SCALAR_WEAVES:
                 quantise(c)
+        gather(EARLY, 5)
         gather(LATE, 5)
         gather(LATE, 6)
         weave(5)
         quantise(4)
+        gather(EARLY, 7)
+        quantise(5)
         gather(LATE, 7)
         weave(6)
-        quantise(5)
         weave(7)
         quantise(6)
         quantise(7)
 
         turn = (0, 1, 4, 5, 2, 3, 6, 7)
-        units = [(j, 0, BANK) for j in range(4)] + [(j, BANK, BANK) for j in range(3)]
-        units += [(0, 2 * BANK, BANK), (0, 6 * CHUNK, CHUNK), (0, 7 * CHUNK, CHUNK), (3, BANK, BANK)]
-        units += [(j, q * BANK, BANK) for j in (1, 2, 3) for q in (2, 3)]
-        for k, (j, s0, n) in enumerate(units):
-            second_product(j, s0, n, turn[k % 8], nc.vector.tensor_copy if n == CHUNK else nc.scalar.copy)
+        for q in range(3):
+            for j in range(4):
+                second_product(j, q * BANK, BANK, turn[(4 * q + j) % 8], nc.scalar.copy)
+        for k, (c, j) in enumerate([(c, j) for j in (0, 1) for c in (6, 7)]):
+            second_product(j, c * CHUNK, CHUNK, turn[4 + k], nc.vector.tensor_copy)
+        for j in (2, 3):
+            second_product(j, 3 * BANK, BANK, turn[j - 2], nc.scalar.copy)
+        turn = [turn[k] for k in (1, 2, 3, 4, 5, 6, 7, 0)]
 
         out_rows = out_0.rearrange("(p t) w -> p t w", t=4)
         out_tiles = out_0.rearrange("(j p) w -> p j w", j=4)
@@ -261,7 +265,7 @@ def tile_moe_sup_glu_relu_kernel(
         def own_choice(r, b0, b1, banks, tag=""):
             turned = {b: bank(which) for b, which in zip(range(b0, b1), banks)}
             for j in (3, 0, 1, 2):
-                picked = held(f"picked{b0}_{r}_{j}", [P, (b1 - b0) * P], F32, tag=tag and f"{tag}_{j}")
+                picked = held(f"picked{b0}_{r}_{j}", [P, (b1 - b0) * P], F32, tag=tag.replace("{}", str(j)) if tag and (r, j) != (1, 3) else "")
                 nc.scalar.activation(picked[:], lookup(j, r, b0 * P, (b1 - b0) * P), COPY)
                 for b in range(b0, b1):
                     nc.tensor.transpose(
@@ -288,7 +292,12 @@ def tile_moe_sup_glu_relu_kernel(
                     )
             return back
 
+        rounded = held("rounded", [P, 4 * T], BF16, tag="y0")
+        rounded_first = held("rounded_first", [P, P, 4], BF16)
+
         def own_store(b, back):
+            if b == 0:
+                nc.scalar.copy(rounded_first[:], back[:].rearrange("p (t w) -> p w t", t=4))
             nc.scalar.copy(results[b][:], back[:].rearrange("p (t w) -> p t w", t=4))
             nc.sync.dma_start(out_rows[:, :, b * P : (b + 1) * P], results[b][:])
 
@@ -297,14 +306,18 @@ def tile_moe_sup_glu_relu_kernel(
             for b in range(2):
                 own_deal(b, r, turned[r][b])
         backs = [own_back(b, turn[1 + b]) for b in range(2)]
-        turned = [own_choice(0, 2, 3, turn[5:6], "picked0_1"), own_choice(1, 2, 3, turn[6:7], "picked0_1")]
+        turned = [own_choice(r, 2, 3, turn[5 + r : 6 + r], f"picked0_{1 - r}_{{}}") for r in range(2)]
         for b in range(2):
             own_store(b, backs[b])
+        backs.append(bank(turn[7]))
         for r in range(2):
             own_deal(2, r, turned[r][2])
-        backs.append(own_back(2, turn[7]))
+            for t in range(4):
+                nc.tensor.matmul(
+                    backs[2][:, P * t : P * (t + 1)], scaled[2][r][:, t, :], ident[:],
+                    is_transpose=True, start=(r, t) == (0, 0), stop=(r, t) == (1, 3),
+                )
 
-        rounded = held("rounded", [P, 4 * T], BF16, tag="y0")
         tail_terms = held("tail_terms", [P, 2, 2, 4, P], F32, tag="picked0_0_3")
         tail_total = held("tail_total", [P, 4, 2 * P], F32)
 
@@ -316,10 +329,15 @@ def tile_moe_sup_glu_relu_kernel(
                 tail_total[:, j0:j1, a * P : (a + 1) * P], tail_terms[:, a, 0, j0:j1, :], tail_terms[:, a, 1, j0:j1, :], ADD
             )
 
-        def tail_turn(a, dealt, j0, j1, which):
+        def tail_turn(a, dealt, j0, j1, which, added=True):
             turned = bank(which)
             for j in range(j0, j1):
-                nc.tensor.transpose(turned[:, P * j : P * (j + 1)], tail_total[:, j, a * P : (a + 1) * P], ident[:])
+                parts = [tail_total[:, j, a * P : (a + 1) * P]] if added else [tail_terms[:, a, r, j, :] for r in range(2)]
+                for r, part in enumerate(parts):
+                    nc.tensor.matmul(
+                        turned[:, P * j : P * (j + 1)], part, ident[:],
+                        is_transpose=True, start=(r == 0), stop=(r == len(parts) - 1),
+                    )
             nc.scalar.copy(
                 dealt[:, :, 32 * j0 : 32 * j1, :],
                 turned[:, P * j0 : P * j1].rearrange("p (m u e) -> p u m e", u=2, e=2),
@@ -351,10 +369,12 @@ def tile_moe_sup_glu_relu_kernel(
         tail_add(1, 3, 4)
         nc.sync.dma_start(out_tiles[:, :, (last - 1) * P :], tail_total[:])
         dealts = [held(f"dealt_pairs{a}", [P, 2, P, 2], BF16) for a in range(2)]
-        tail_turn(0, dealts[0], 0, 4, turn[1])
+        tail_turn(0, dealts[0], 0, 4, turn[5])
+        rounded_second = held("rounded_second", [P, P, 4], BF16, tag=f"gate_col{OWN - 1}_1")
+        nc.scalar.copy(rounded_second[:], backs[1][:].rearrange("p (t w) -> p w t", t=4))
         own_store(2, backs[2])
-        tail_turn(1, dealts[1], 0, 3, turn[2])
-        tail_turn(1, dealts[1], 3, 4, turn[5])
+        tail_turn(1, dealts[1], 0, 3, turn[6])
+        tail_turn(1, dealts[1], 3, 4, turn[5], added=False)
         tail_back(0, dealts[0], turn[3])
         tail_back(1, dealts[1], turn[4])
 
@@ -367,20 +387,26 @@ def tile_moe_sup_glu_relu_kernel(
                 rows.rearrange("p t (c i) -> p c t i", i=4),
             )
 
-        def planes_of(t0, n):
+        def planes_of(t0, n, values=None):
             cols = slice(t0, t0 + n)
             nc.vector.quantize_mx(
-                out=out_codes[:, cols].bitcast(FP8X4), scales=out_plane[:, cols], in_=rounded[:, 4 * t0 : 4 * (t0 + n)],
+                out=out_codes[:, cols].bitcast(FP8X4), scales=out_plane[:, cols], in_=rounded[:, 4 * t0 : 4 * (t0 + n)] if values is None else values,
             )
-            nc.sync.dma_start(out_words[:, cols], out_codes[:, cols].bitcast(I32))
+
+        def store_codes(t0, t1):
+            nc.sync.dma_start(out_words[:, t0:t1], out_codes[:, t0:t1].bitcast(I32))
 
         round_rows(regrouped[:], first, width)
-        round_rows(results[0][:], 0, P)
+        planes_of(0, P, rounded_first[:].rearrange("p w t -> p (w t)"))
         planes_of(first, width)
-        for b in range(1, OWN):
-            round_rows(results[b][:], b * P, P)
-        planes_of(0, OWN * P)
-        planes_of((last - 1) * P, 2 * P)
+        store_codes(first, first + width)
+        planes_of(P, P, rounded_second[:].rearrange("p w t -> p (w t)"))
+        round_rows(results[2][:], 2 * P, P)
+        planes_of((last - 1) * P, P)
+        planes_of(2 * P, P)
+        store_codes(0, first)
+        planes_of(last * P, P)
+        store_codes((last - 1) * P, T)
         scale_rows = out_2[0].bitcast(I32).rearrange("(q r) n -> r q n", r=4)
         for r in range(4):
             (nc.scalar if r < 3 else nc.sync).dma_start(scale_rows[r], out_plane[r:P:32, :].bitcast(I32))

from contextlib import ExitStack

import concourse.mybir as mybir
from concourse.masks import make_identity

K, T, E, C, H, N = 512, 1024, 16, 128, 512, 512
S = E * C
FLOPS = 2 * 2 * K * H * T + 2 * H * N * S

F32 = mybir.dt.float32
BF16 = mybir.dt.bfloat16
I32 = mybir.dt.int32
U32 = mybir.dt.uint32
U16 = mybir.dt.uint16
U8 = mybir.dt.uint8
FP8X4 = mybir.dt.float8_e4m3fn_x4
FP4X4 = mybir.dt.float4_e2m1fn_x4
MULT = mybir.AluOpType.mult
ADD = mybir.AluOpType.add
MAX = mybir.AluOpType.max
RELU = mybir.ActivationFunctionType.Relu
COPY = mybir.ActivationFunctionType.Copy

P = 128
BANK = 512
STEP = BANK // 2
AHEAD = 2
CHUNK = 256
EARLY, LATE = 1, 0
GPSIMD_STEPS = 3
SCALAR_WEAVES = 5
OWN = 3
ROUND = 3


def tile_moe_sup_glu_relu_kernel(
    tc, x_words, x_scales, w1_words, w1_scales, w3_words, w3_scales, w2_words, w2_scales,
    gate, offs, pos1, pos2, out_0, out_1, out_2,
):
    nc = tc.nc
    with ExitStack() as ctx:
        keep = ctx.enter_context(tc.tile_pool(name="keep", bufs=1))
        psum = ctx.enter_context(tc.psum_pool(name="psum", bufs=1))

        def held(name, shape, dtype, tag=""):
            return keep.tile(shape, dtype, name=name, tag=tag or name, align_bytes=64)

        def bank(i):
            return psum.tile([P, BANK], F32, name=f"bank{i}")

        def load_scale_rows(plane, rows, which=range(4)):
            for r in which:
                dst = plane[r:P:32, :].bitcast(I32)
                src = rows[r]
                if len(src.shape) == 3:
                    dst = dst.rearrange("q (e n) -> q e n", e=src.shape[1])
                nc.sync.dma_start(dst, src)

        w3s_raw = held("w3s_raw", [P, H], U8)
        w1s_raw = held("w1s_raw", [P, H], U8)
        xs = held("xs", [P, T], U8)
        w2s = held("w2s", [P, E * N], U8)
        nc.gpsimd.memset(w3s_raw[:].bitcast(I32), 0)
        nc.gpsimd.memset(w1s_raw[:].bitcast(I32), 0)

        w3_raw = held("w3_raw", [P, H], I32)
        w1_raw = held("w1_raw", [P, H], I32)
        xw = [held(f"xw{a}", [P, T // 2], I32) for a in range(2)]
        xs_rows = x_scales[0].bitcast(I32).rearrange("(q r) n -> r q n", r=4)
        x_all = x_words[0].rearrange("p t d -> p (t d)").bitcast(I32)
        load_scale_rows(xs, xs_rows, (0, 1))
        load_scale_rows(w3s_raw, w3_scales[0].bitcast(I32).rearrange("(q r) n -> r q n", r=4))
        nc.sync.dma_start(w3_raw[:], w3_words[0].rearrange("p i d -> p (i d)").bitcast(I32))
        nc.sync.dma_start(xw[0][:], x_all[:, : T // 2])
        load_scale_rows(xs, xs_rows, (2, 3))
        nc.sync.dma_start(w1_raw[:], w1_words[0].rearrange("p i d -> p (i d)").bitcast(I32))
        load_scale_rows(w1s_raw, w1_scales[0].bitcast(I32).rearrange("(q r) n -> r q n", r=4))
        nc.sync.dma_start(xw[1][:], x_all[:, T // 2 :])
        offs_t = held("offs_t", [P, S // 16], U16)
        nc.sync.dma_start(offs_t[:], offs)
        w2w = [held(f"w2w{a}", [P, 4 * 2 * N], U8) for a in range(4)]
        for a in range(4):
            nc.sync.dma_start(
                w2w[a][:].bitcast(I32).rearrange("p (e c) -> p e c", e=4),
                w2_words[4 * a : 4 * a + 4].bitcast(I32).rearrange("e s p c -> p (e s) c"),
            )
        load_scale_rows(w2s, w2_scales.bitcast(I32).rearrange("e s (q r) n -> r q (e s) n", r=4))
        pos_t = [held(f"pos{r}", [P, T // 16], U16) for r in range(2)]
        nc.sync.dma_start(pos_t[0][:], pos1)
        nc.sync.dma_start(pos_t[1][:], pos2)
        gate_t = [held(f"gate{r}", [P, T - OWN * P], F32) for r in range(2)]
        gate_col = [[held(f"gate_col{b}_{r}", [P, 1], F32) for r in range(2)] for b in range(OWN)]
        for r in range(2):
            nc.sync.dma_start(gate_t[r][:], gate[r, :, OWN * P :])
        for r in range(2):
            for b in range(OWN):
                nc.sync.dma_start(gate_col[b][r][:], gate[r, 0, b * P : (b + 1) * P].rearrange("(p o) -> p o", o=1))

        w3 = held("w3", [P, H], I32)
        w1 = held("w1", [P, H], I32)
        w3s = held("w3s", [P, H], U8)
        w1s = held("w1s", [P, H], U8)
        for operand in (((w3, w3_raw, 4), (w3s, w3s_raw, 16)), ((w1, w1_raw, 4), (w1s, w1s_raw, 16))):
            for u in (EARLY, LATE):
                for dst, src, run in operand:
                    nc.vector.tensor_copy(
                        dst[:].rearrange("p (t c i) -> p c t i", t=4, i=run)[:, :, 2 * u : 2 * u + 2, :],
                        src[:].rearrange("p (c i t) -> p c t i", t=4, i=run)[:, :, 2 * u : 2 * u + 2, :],
                    )

        h = [held(f"h{u}", [P, 2 * T], BF16) for u in range(2)]

        def first_product(w, ws, u, tok, acc):
            for e in range(2):
                cols = slice(P * (2 * u + e), P * (2 * u + e + 1))
                nc.tensor.matmul_mx(
                    out=acc[:, STEP * e : STEP * (e + 1)],
                    lhsT=w[:, cols].bitcast(FP8X4),
                    lhsT_scale=ws[:, cols],
                    rhs=xw[tok // (T // 2)][:, tok % (T // 2) : tok % (T // 2) + STEP].bitcast(FP8X4),
                    rhs_scale=xs[:, tok : tok + STEP],
                    start=True,
                    stop=True,
                )
            return acc[:].rearrange("p (e t) -> p t e", e=2)

        steps = [(EARLY, tok) for tok in range(0, T, STEP)] + [(LATE, (tok + T // 2) % T) for tok in range(0, T, STEP)]
        half = len(steps) // 2
        step_banks = [(i, half + i) for i in range(half)] + [(i, i + 1) for i in (0, 4, 2, 6)]
        a3_sb = [held(f"a3_sb{i}", [P, STEP, 2], F32) for i in range(len(steps))]

        def linear_half(i):
            nc.scalar.copy(a3_sb[i][:], first_product(w3, w3s, *steps[i], bank(step_banks[i][0])))

        def gated_half(i):
            u, tok = steps[i]
            a1 = first_product(w1, w1s, u, tok, bank(step_banks[i][1]))
            out = h[u][:, 2 * tok : 2 * (tok + STEP)].rearrange("p (t e) -> p t e", e=2)
            if half <= i < half + GPSIMD_STEPS:
                a1_sb = held(f"a1_sb{i}", [P, STEP, 2], F32)
                nc.scalar.activation(a1_sb[:], a1, RELU)
                nc.gpsimd.tensor_tensor(out, a1_sb[:], a3_sb[i][:], MULT)
            else:
                nc.vector.scalar_tensor_tensor(
                    out=out, in0=a1, scalar=0.0, in1=a3_sb[i][:], op0=MAX, op1=MULT,
                )

        for i in range(AHEAD):
            linear_half(i)
        for i in range(len(steps)):
            if i >= AHEAD:
                linear_half(i)
            gated_half(i)

        ident = held("ident", [P, P], F32, tag=f"a1_sb{half + GPSIMD_STEPS - 1}")
        make_identity(nc, ident[:])

        places = [(0, 1), (3, 4), (7, 8), (1, 2), (4, 5), (1, 2), (5, 6), (1, 2)]
        pairs = held("pairs", [P, 9 * CHUNK], U32)
        y = [held(f"y{j}", [P, S], F32) for j in range(4)]
        woven = {}
        codes = {}
        planes = {}

        def gather(u, c):
            place = places[c][u]
            nc.vector.tensor_copy(
                pairs[:, place * CHUNK : (place + 1) * CHUNK],
                h[u][:].bitcast(U32).indirect(offs_t[:, c * CHUNK // 16 : (c + 1) * CHUNK // 16]),
            )

        def weave(c):
            woven[c] = pairs[:, 3 * CHUNK : 5 * CHUNK] if c == 5 else held(f"woven{c}", [P, 2 * CHUNK], U32)[:]
            late, early = places[c]
            copy = nc.scalar.copy if c < SCALAR_WEAVES else nc.vector.tensor_copy
            copy(
                woven[c].rearrange("p (s u) -> p s u", u=2),
                pairs[:].rearrange("p (k s) -> p s k", s=CHUNK)[:, :, late : early + 1 : early - late],
            )

        def quantise(c):
            codes[c] = held(f"codes{c}", [P, CHUNK], U32)
            planes[c] = held(f"planes{c}", [P, CHUNK], U8)
            nc.vector.quantize_mx(out=codes[c][:].bitcast(FP8X4), scales=planes[c][:], in_=woven[c].bitcast(BF16))

        def second_product(j, s0, n, which, copy):
            acc = bank(which)
            for s in range(s0, s0 + n, C):
                e = s // C
                c, o = divmod(s, CHUNK)
                w0 = (e % 4) * 2 * N + 2 * P * j
                nc.tensor.matmul_mx(
                    out=acc[:, s - s0 : s - s0 + C],
                    lhsT=w2w[e // 4][:, w0 : w0 + 2 * P].bitcast(FP4X4),
                    lhsT_scale=w2s[:, e * N + P * j : e * N + P * (j + 1)],
                    rhs=codes[c][:, o : o + C].bitcast(FP8X4),
                    rhs_scale=planes[c][:, o : o + C],
                    start=True,
                    stop=True,
                )
            copy(y[j][:, s0 : s0 + n], acc[:, :n])

        for c in (0, 1, 2, 3, 4, 6):
            gather(EARLY, c)
        for c in range(3):
            gather(LATE, c)
        for c in range(SCALAR_WEAVES):
            weave(c)
            if c + 3 < SCALAR_WEAVES:
                gather(LATE, c + 3)
            if c + 1 < SCALAR_WEAVES:
                quantise(c)
        gather(EARLY, 5)
        gather(LATE, 5)
        gather(LATE, 6)
        weave(5)
        quantise(4)
        gather(EARLY, 7)
        quantise(5)
        gather(LATE, 7)
        weave(6)
        weave(7)
        quantise(6)
        quantise(7)

        turn = (0, 1, 4, 5, 2, 3, 6, 7)
        for q in range(3):
            for j in range(4):
                second_product(j, q * BANK, BANK, turn[(4 * q + j) % 8], nc.scalar.copy)
        for k, (c, j) in enumerate([(c, j) for j in (0, 1) for c in (6, 7)]):
            second_product(j, c * CHUNK, CHUNK, turn[4 + k], nc.vector.tensor_copy)
        for j in (2, 3):
            second_product(j, 3 * BANK, BANK, turn[j - 2], nc.scalar.copy)
        turn = [turn[k] for k in (1, 2, 3, 4, 5, 6, 7, 0)]

        out_rows = out_0.rearrange("(p t) w -> p t w", t=4)
        out_tiles = out_0.rearrange("(j p) w -> p j w", j=4)
        out_words = out_1[0].rearrange("p t d -> p (t d)").bitcast(I32)
        blocks = T // P
        last = blocks - 1

        def lookup(j, r, t0, n):
            return y[j][:].indirect(pos_t[r][:, t0 // 16 : (t0 + n) // 16])

        def gated(out, j, r, t0, n):
            nc.vector.tensor_tensor(out, lookup(j, r, t0, n), gate_t[r][:, t0 - OWN * P : t0 - OWN * P + n], MULT)

        first = OWN * P
        width = ROUND * P
        cut = width - P
        for j in range(4):
            terms = [held(f"round_terms{j}_{r}", [P, width], F32) for r in range(2)]
            total = held(f"round_total{j}", [P, width], F32)
            gated(terms[0][:], j, 0, first, width)
            for t0, n in ((0, cut), (cut, P)):
                gated(terms[1][:, t0 : t0 + n], j, 1, first + t0, n)
            for t0, n in ((0, cut), (cut, P)):
                nc.vector.tensor_tensor(total[:, t0 : t0 + n], terms[0][:, t0 : t0 + n], terms[1][:, t0 : t0 + n], ADD)
            nc.sync.dma_start(out_tiles[:, j, first : first + width], total[:])
        regrouped = held("regrouped", [P, 4, width], F32)
        nc.sync.dma_start(regrouped[:], out_rows[:, :, first : first + width])

        scaled = [[held(f"scaled{b}_{r}", [P, 4, P], F32) for r in range(2)] for b in range(OWN)]

        def own_choice(r, b0, b1, banks, tag=""):
            turned = {b: bank(which) for b, which in zip(range(b0, b1), banks)}
            for j in (3, 0, 1, 2):
                picked = held(f"picked{b0}_{r}_{j}", [P, (b1 - b0) * P], F32, tag=tag.replace("{}", str(j)) if tag and (r, j) != (1, 3) else "")
                nc.scalar.activation(picked[:], lookup(j, r, b0 * P, (b1 - b0) * P), COPY)
                for b in range(b0, b1):
                    nc.tensor.transpose(
                        turned[b][:, P * j : P * (j + 1)], picked[:, (b - b0) * P : (b - b0 + 1) * P], ident[:]
                    )
            return turned

        def own_deal(b, r, turned):
            nc.scalar.activation(
                scaled[b][r][:].rearrange("p t (c i) -> p c t i", i=4),
                turned[:].rearrange("p (c i t) -> p c t i", t=4, i=4),
                COPY, scale=gate_col[b][r][:],
            )

        results = [held(f"result{b}", [P, 4, P], F32) for b in range(OWN)]

        def own_back(b, which):
            back = bank(which)
            for t in range(4):
                for r in range(2):
                    nc.tensor.matmul(
                        back[:, P * t : P * (t + 1)], scaled[b][r][:, t, :], ident[:],
                        is_transpose=True, start=(r == 0), stop=(r == 1),
                    )
            return back

        rounded = held("rounded", [P, 4 * T], BF16, tag="y0")
        rounded_first = held("rounded_first", [P, P, 4], BF16)

        def own_store(b, back):
            if b == 0:
                nc.scalar.copy(rounded_first[:], back[:].rearrange("p (t w) -> p w t", t=4))
            nc.scalar.copy(results[b][:], back[:].rearrange("p (t w) -> p t w", t=4))
            nc.sync.dma_start(out_rows[:, :, b * P : (b + 1) * P], results[b][:])

        turned = [own_choice(r, 0, 2, turn[1 + 2 * r : 3 + 2 * r]) for r in range(2)]
        for r in range(2):
            for b in range(2):
                own_deal(b, r, turned[r][b])
        backs = [own_back(b, turn[1 + b]) for b in range(2)]
        turned = [own_choice(r, 2, 3, turn[5 + r : 6 + r], f"picked0_{1 - r}_{{}}") for r in range(2)]
        for b in range(2):
            own_store(b, backs[b])
        backs.append(bank(turn[7]))
        for r in range(2):
            own_deal(2, r, turned[r][2])
            for t in range(4):
                nc.tensor.matmul(
                    backs[2][:, P * t : P * (t + 1)], scaled[2][r][:, t, :], ident[:],
                    is_transpose=True, start=(r, t) == (0, 0), stop=(r, t) == (1, 3),
                )

        tail_terms = held("tail_terms", [P, 2, 2, 4, P], F32, tag="picked0_0_3")
        tail_total = held("tail_total", [P, 4, 2 * P], F32)

        def tail_gather(a, j, r):
            gated(tail_terms[:, a, r, j, :], j, r, (last - 1 + a) * P, P)

        def tail_add(a, j0, j1):
            nc.vector.tensor_tensor(
                tail_total[:, j0:j1, a * P : (a + 1) * P], tail_terms[:, a, 0, j0:j1, :], tail_terms[:, a, 1, j0:j1, :], ADD
            )

        def tail_turn(a, dealt, j0, j1, which, added=True):
            turned = bank(which)
            for j in range(j0, j1):
                parts = [tail_total[:, j, a * P : (a + 1) * P]] if added else [tail_terms[:, a, r, j, :] for r in range(2)]
                for r, part in enumerate(parts):
                    nc.tensor.matmul(
                        turned[:, P * j : P * (j + 1)], part, ident[:],
                        is_transpose=True, start=(r == 0), stop=(r == len(parts) - 1),
                    )
            nc.scalar.copy(
                dealt[:, :, 32 * j0 : 32 * j1, :],
                turned[:, P * j0 : P * j1].rearrange("p (m u e) -> p u m e", u=2, e=2),
            )

        def tail_back(a, dealt, which):
            back = bank(which)
            words = dealt[:].rearrange("p u m e -> p (u m e)").bitcast(F32)
            for u in range(2):
                nc.tensor.transpose(back[:, P * u : P * (u + 1)], words[:, P * u : P * (u + 1)], ident[:])
            b = last - 1 + a
            nc.scalar.copy(
                rounded[:, 4 * P * b : 4 * P * (b + 1)].bitcast(F32).rearrange("p (w u) -> p w u", u=2),
                back[:, : 2 * P].rearrange("p (u w) -> p w u", u=2),
            )

        for j in range(4):
            for r in range(2):
                tail_gather(0, j, r)
        for r in range(2):
            tail_gather(1, 0, r)
        tail_add(0, 0, 4)
        for j in (1, 2):
            for r in range(2):
                tail_gather(1, j, r)
        tail_gather(1, 3, 0)
        tail_add(1, 0, 3)
        tail_gather(1, 3, 1)
        tail_add(1, 3, 4)
        nc.sync.dma_start(out_tiles[:, :, (last - 1) * P :], tail_total[:])
        dealts = [held(f"dealt_pairs{a}", [P, 2, P, 2], BF16) for a in range(2)]
        tail_turn(0, dealts[0], 0, 4, turn[5])
        rounded_second = held("rounded_second", [P, P, 4], BF16, tag=f"gate_col{OWN - 1}_1")
        nc.scalar.copy(rounded_second[:], backs[1][:].rearrange("p (t w) -> p w t", t=4))
        own_store(2, backs[2])
        tail_turn(1, dealts[1], 0, 3, turn[6])
        tail_turn(1, dealts[1], 3, 4, turn[5], added=False)
        tail_back(0, dealts[0], turn[3])
        tail_back(1, dealts[1], turn[4])

        out_codes = held("out_codes", [P, T], U32)
        out_plane = held("out_plane", [P, T], U8)

        def round_rows(rows, t0, n):
            nc.vector.tensor_copy(
                rounded[:, 4 * t0 : 4 * (t0 + n)].rearrange("p (c i t) -> p c t i", t=4, i=4),
                rows.rearrange("p t (c i) -> p c t i", i=4),
            )

        def planes_of(t0, n, values=None):
            cols = slice(t0, t0 + n)
            nc.vector.quantize_mx(
                out=out_codes[:, cols].bitcast(FP8X4), scales=out_plane[:, cols], in_=rounded[:, 4 * t0 : 4 * (t0 + n)] if values is None else values,
            )

        def store_codes(t0, t1):
            nc.sync.dma_start(out_words[:, t0:t1], out_codes[:, t0:t1].bitcast(I32))

        round_rows(regrouped[:], first, width)
        planes_of(0, P, rounded_first[:].rearrange("p w t -> p (w t)"))
        planes_of(first, width)
        store_codes(first, first + width)
        planes_of(P, P, rounded_second[:].rearrange("p w t -> p (w t)"))
        round_rows(results[2][:], 2 * P, P)
        planes_of((last - 1) * P, P)
        planes_of(2 * P, P)
        store_codes(0, first)
        planes_of(last * P, P)
        store_codes((last - 1) * P, T)
        scale_rows = out_2[0].bitcast(I32).rearrange("(q r) n -> r q n", r=4)
        for r in range(4):
            (nc.scalar if r < 3 else nc.sync).dma_start(scale_rows[r], out_plane[r:P:32, :].bitcast(I32))
